import numpy as np
import ml_dtypes


def mxq(x, axis, fmt="e4m3"):
    dtype, down = {"e4m3": (ml_dtypes.float8_e4m3fn, 7), "e5m2": (ml_dtypes.float8_e5m2, 14)}[fmt]
    v = np.moveaxis(np.asarray(x, np.float32).astype(ml_dtypes.bfloat16).astype(np.float64), axis, -1)
    blocks = v.reshape(v.shape[:-1] + (-1, 32))
    amax = np.abs(blocks).max(-1, keepdims=True)
    byte = np.maximum(np.where(amax > 0, np.frexp(amax)[1] - 1 + 127, 0) - down, 1)
    scale = np.exp2(byte - 127.0)
    codes = (blocks / scale).astype(np.float32).astype(dtype).astype(np.float64)
    return np.moveaxis((codes * scale).reshape(v.shape), -1, axis)


WIDE = False


def mx_kscale(k):
    if not WIDE:
        return np.ones(k)
    levels = np.array([24, -24, 12, -12, 0])
    if k % 512:
        return np.exp2(np.random.permutation(np.resize(levels, k // 32))).repeat(32)
    a = np.empty((k // 512, 16))
    for p in range(k // 512):
        a[p, :8] = np.random.permutation(np.resize(levels, 8))
        for g in range(8):
            far = levels[np.abs(levels - a[p, g]) >= 10]
            a[p, g + 8] = far[np.random.randint(len(far))]
    return np.exp2(a.ravel()).repeat(32)


def f64(x):
    return np.asarray(x).astype(np.float64)


def striped(idx):
    return np.tile(idx.reshape(-1, 16).T, (8, 1)).astype(np.uint16)


def unstriped(offs):
    return offs[:16].T.reshape(-1).astype(np.int64)


E2M1 = np.array([0.0, 0.5, 1.0, 1.5, 2.0, 3.0, 4.0, 6.0, -0.0, -0.5, -1.0, -1.5, -2.0, -3.0, -4.0, -6.0])


def pack_weight(w, fmt):
    k, n = w.shape
    w = f64(np.asarray(w, np.float32).astype(ml_dtypes.bfloat16)).reshape(k // 32, 32, n)
    amax = np.abs(w).max(1)
    if fmt == "e4m3":
        byte = np.frexp(amax)[1] - 1 + 127 - 7
    else:
        mant, ex = np.frexp(amax / 6.0)
        byte = np.where(mant > 0.5, ex, ex - 1) + 127
    byte = np.clip(np.where(amax > 0, byte, 1), 1, 254)
    scaled = (w * np.exp2(127.0 - byte)[:, None, :]).reshape(k, n).astype(np.float32)
    by_word = np.ascontiguousarray(scaled.reshape(k // 512, 128, 4, n).transpose(0, 1, 3, 2))
    if fmt == "e4m3":
        words = by_word.astype(ml_dtypes.float8_e4m3fn).view(np.uint8)
    else:
        c = by_word.astype(ml_dtypes.float4_e2m1fn).view(np.uint8) & 0xF
        words = (c[..., 0::2] | (c[..., 1::2] << 4)).reshape(k // 512, 128, 2 * n)
    return np.ascontiguousarray(words), np.ascontiguousarray(byte.astype(np.uint8).reshape(k // 512, 16, n))


def unpack_weight(words, scales, fmt):
    g, _, n = scales.shape
    words = np.ascontiguousarray(words).reshape(g, 128, n, -1)
    if fmt == "e4m3":
        vals = words.view(ml_dtypes.float8_e4m3fn).astype(np.float64)
    else:
        nib = np.empty((g, 128, n, 4), np.uint8)
        nib[..., 0::2] = words & 0xF
        nib[..., 1::2] = words >> 4
        vals = E2M1[nib]
    vals = vals * np.repeat(np.exp2(scales.astype(np.float64) - 127.0), 8, axis=1)[..., None]
    return vals.transpose(0, 1, 3, 2).reshape(g * 512, n)


K, M, N, J, T = 512, 1024, 256, 2048, 4096


def setup_inputs():
    n = np.random.standard_normal
    s = mx_kscale(K)[:, None]
    u = mx_kscale(J)[:, None]
    p_tab = pack_weight(0.5 * n((K, T)) / np.sqrt(K) / s, "e4m3")
    p_al = pack_weight(n((J, N)) / np.sqrt(J) / u, "e4m3")
    return {
        "x": (n((K, M)) * s).astype(np.float32),
        "tab_words": p_tab[0],
        "tab_scales": p_tab[1],
        "cw": (np.random.uniform(0.5, 2.0, J) * u[:, 0]).astype(np.float32),
        "cb": (0.3 * n(J)).astype(np.float32),
        "al_words": p_al[0],
        "al_scales": p_al[1],
        "offs": striped(np.random.permutation(T)[:J]),
    }


def reference(x, tab_words, tab_scales, cw, cb, al_words, al_scales, offs):
    idx = unstriped(offs)
    x_ = mxq(f64(x), 0, "e4m3")
    tab_ = unpack_weight(tab_words, tab_scales, "e4m3")[:, idx]
    d = tab_.T @ x_
    h = f64(cw)[:, None] * np.maximum(d + f64(cb)[:, None], 0.0)
    h_ = mxq(h, 0, "e4m3")
    al_ = unpack_weight(al_words, al_scales, "e4m3")
    y = al_.T @ h_
    return y

@@ -1,0 +1,183 @@
+from contextlib import ExitStack
+
+import concourse.mybir as mybir
+
+K, M, N, J, T = 512, 1024, 256, 2048, 4096
+FLOPS = 2 * K * M * J + 2 * J * M * N
+
+F32 = mybir.dt.float32
+BF16 = mybir.dt.bfloat16
+I32 = mybir.dt.int32
+U32 = mybir.dt.uint32
+U16 = mybir.dt.uint16
+U8 = mybir.dt.uint8
+FP8X4 = mybir.dt.float8_e4m3fn_x4
+ALU = mybir.AluOpType
+ACT = mybir.ActivationFunctionType
+
+P = 128
+PACK = 4
+PASS = P * PACK
+JB = J // PASS
+HALF = 512
+HALVES = M // HALF
+NT = N // P
+
+
+def tile_list_kernl_arc_none_kernel(
+    tc, x, tab_words, tab_scales, cw, cb, al_words, al_scales, offs, out
+):
+    nc = tc.nc
+    with ExitStack() as ctx:
+        keep = ctx.enter_context(tc.tile_pool(name="keep", bufs=1))
+        ring = ctx.enter_context(tc.tile_pool(name="ring", bufs=3))
+        xring = ctx.enter_context(tc.tile_pool(name="xring", bufs=2))
+        dpsum = ctx.enter_context(tc.psum_pool(name="dpsum", bufs=6))
+        ypsum = ctx.enter_context(tc.psum_pool(name="ypsum", bufs=1))
+
+        offsets = keep.tile([P, J // 16], U16, name="offsets")
+        nc.sync.dma_start(offsets[:], offs)
+
+        tab_s = keep.tile([P, T // 4], I32, name="tab_s", align_bytes=64)
+        nc.vector.memset(tab_s[:], 0)
+        for q in range(4):
+            nc.scalar.dma_start(tab_s[32 * q : 32 * q + 4, :], tab_scales[0, 4 * q : 4 * q + 4, :].bitcast(I32))
+
+        cw_sb = keep.tile([P, JB, PACK], F32, name="cw_sb")
+        cb_sb = keep.tile([P, JB, PACK], F32, name="cb_sb")
+        nc.sync.dma_start(cw_sb[:], cw.rearrange("(b p t) -> p b t", b=JB, t=PACK))
+        nc.sync.dma_start(cb_sb[:], cb.rearrange("(b p t) -> p b t", b=JB, t=PACK))
+        al_s = keep.tile([P, N // 4], I32, name="al_s", align_bytes=64)
+        nc.gpsimd.memset(al_s[:], 0)
+        for q in range(4):
+            nc.gpsimd.dma_start(al_s[32 * q : 32 * q + 16, :], al_scales[:, 4 * q : 4 * q + 4, :].bitcast(I32))
+
+        x_raw = []
+        for h in range(HALVES):
+            x_raw.append(xring.tile([P, PACK, HALF], F32, name="x_raw"))
+        x_rows = x.rearrange("(p t) m -> p t m", t=PACK)
+        nc.sync.dma_start(x_raw[0][:], x_rows[:, :, 0:HALF])
+        tab_w = keep.tile([P, T], I32, name="tab_w", align_bytes=64)
+        nc.sync.dma_start(tab_w[:], tab_words[0].rearrange("p t i -> p (t i)").bitcast(I32))
+        nc.sync.dma_start(x_raw[1][:], x_rows[:, :, HALF:M])
+        al_w = keep.tile([P, JB, N], I32, name="al_w", align_bytes=64)
+        nc.sync.dma_start(al_w[:], al_words.rearrange("a p n i -> p a (n i)").bitcast(I32))
+
+        sign = keep.tile([P, JB, PACK], F32, name="sign")
+        mag = keep.tile([P, JB, PACK], F32, name="mag")
+        bias = keep.tile([P, JB, PACK], F32, name="bias")
+        nc.gpsimd.tensor_scalar(mag[:], cw_sb[:], 0.0, 2.0, ALU.is_ge, ALU.mult)
+        nc.gpsimd.tensor_scalar(sign[:], mag[:], 1.0, -1.0, ALU.mult, ALU.add)
+        nc.gpsimd.tensor_tensor(mag[:], cw_sb[:], sign[:], ALU.mult)
+        nc.gpsimd.tensor_tensor(bias[:], mag[:], cb_sb[:], ALU.mult)
+
+        v_s = keep.tile([P, JB, PACK, P], U8, name="v_s", align_bytes=64)
+        x_w = keep.tile([P, M], U32, name="x_w", align_bytes=64)
+
+        cols_per_pass = PASS // 16
+        picked = []
+        for b0, shared in ((0, "early_a"), (2, "early_b")):
+            picked_s = keep.tile([P, 2 * PASS], U8, name="picked_s", tag=shared, align_bytes=64)
+            nc.vector.tensor_copy(
+                picked_s[:],
+                tab_s[:].bitcast(U8).indirect(offsets[:, b0 * cols_per_pass : (b0 + 2) * cols_per_pass]),
+            )
+            picked.append((b0, picked_s))
+        for b0, picked_s in picked:
+            nc.vector.tensor_copy(v_s[:, b0 : b0 + 2], picked_s[:].rearrange("p (b c t) -> p b t c", b=2, t=PACK))
+        x_s = keep.tile([P, M], U8, name="x_s", tag="early_a", align_bytes=64)
+        v_w = keep.tile([P, JB, PACK, P], U32, name="v_w", tag="early_b", align_bytes=64)
+
+        def round_x(h):
+            x_bf = xring.tile([P, HALF, PACK], BF16, name="x_bf", align_bytes=64)
+            nc.scalar.copy(
+                x_bf[:].rearrange("p (c i) t -> p c t i", i=4),
+                x_raw[h][:].rearrange("p t (c i) -> p c t i", i=4),
+            )
+            return x_bf
+
+        def quantise_x(h, x_bf):
+            cols = slice(h * HALF, (h + 1) * HALF)
+            nc.vector.quantize_mx(
+                out=x_w[:, cols].bitcast(FP8X4), scales=x_s[:, cols], in_=x_bf[:].rearrange("p m t -> p (m t)")
+            )
+
+        quantise_x(0, round_x(0))
+        x_next = round_x(1)
+
+        for b in range(JB):
+            nc.vector.tensor_copy(
+                v_w[:, b].rearrange("p t c -> p c t"),
+                tab_w[:].bitcast(U32).indirect(offsets[:, b * cols_per_pass : (b + 1) * cols_per_pass]),
+            )
+
+        quantise_x(1, x_next)
+
+        def first_product(h, b):
+            cols = slice(h * HALF, (h + 1) * HALF)
+            h_rows = ring.tile([P, PACK, HALF], BF16, name="h_rows", align_bytes=64)
+            for t in range(PACK):
+                d = dpsum.tile([P, HALF], F32, name="d")
+                nc.tensor.matmul_mx(
+                    out=d[:],
+                    lhsT=v_w[:, b, t, :].bitcast(FP8X4),
+                    lhsT_scale=v_s[:, b, t, :],
+                    rhs=x_w[:, cols].bitcast(FP8X4),
+                    rhs_scale=x_s[:, cols],
+                    start=True,
+                    stop=True,
+                )
+                nc.scalar.activation(
+                    h_rows[:, t, :], d[:], ACT.Relu, bias=bias[:, b, t : t + 1], scale=mag[:, b, t : t + 1]
+                )
+            return h_rows
+
+        def apply_sign(b, h_rows):
+            for t in range(PACK):
+                nc.vector.tensor_scalar(h_rows[:, t, :], h_rows[:, t, :], sign[:, b, t : t + 1], None, ALU.mult)
+
+        def interleave(h_rows):
+            h_bf = ring.tile([P, HALF, PACK], BF16, name="h_bf", align_bytes=64)
+            nc.vector.tensor_copy(
+                h_bf[:].rearrange("p (c i) t -> p c t i", i=4),
+                h_rows[:].rearrange("p t (c i) -> p c t i", i=4),
+            )
+            return h_bf
+
+        y_acc = {}
+
+        def second_product(h, b, h_bf):
+            h_w = ring.tile([P, HALF], U32, name="h_w", align_bytes=64)
+            h_s = ring.tile([P, HALF], U8, name="h_s", align_bytes=64)
+            nc.vector.quantize_mx(out=h_w[:].bitcast(FP8X4), scales=h_s[:], in_=h_bf[:].rearrange("p m t -> p (m t)"))
+            for n in range(NT):
+                if b == 0:
+                    y_acc[n] = ypsum.tile([P, HALF], F32, name="y%d" % n)
+                rows = slice(n * P, (n + 1) * P)
+                nc.tensor.matmul_mx(
+                    out=y_acc[n][:],
+                    lhsT=al_w[:, b, rows].bitcast(FP8X4),
+                    lhsT_scale=al_s[:].bitcast(U8)[4 * b :, rows],
+                    rhs=h_w[:].bitcast(FP8X4),
+                    rhs_scale=h_s[:],
+                    start=(b == 0),
+                    stop=(b == JB - 1),
+                )
+            if b == JB - 1:
+                for n in range(NT):
+                    y_sb = xring.tile([P, HALF], F32, name="y_sb%d" % n)
+                    if h == HALVES - 1 and n == NT - 1:
+                        nc.vector.tensor_copy(y_sb[:], y_acc[n][:])
+                    else:
+                        nc.scalar.copy(y_sb[:], y_acc[n][:])
+                    nc.sync.dma_start(out[n * P : (n + 1) * P, h * HALF : (h + 1) * HALF], y_sb[:])
+
+        pending = None
+        for h in range(HALVES):
+            for b in range(JB):
+                h_rows = first_product(h, b)
+                apply_sign(b, h_rows)
+                if pending is not None:
+                    second_product(*pending)
+                pending = (h, b, interleave(h_rows))
+        second_product(*pending)

@@ -38,19 +38,17 @@ def tile_list_kernl_arc_none_kernel(
         offsets = keep.tile([P, J // 16], U16, name="offsets")
         nc.sync.dma_start(offsets[:], offs)
 
-        tab_s = keep.tile([P, T // 4], I32, name="tab_s", align_bytes=64)
-        nc.vector.memset(tab_s[:], 0)
-        for q in range(4):
-            nc.scalar.dma_start(tab_s[32 * q : 32 * q + 4, :], tab_scales[0, 4 * q : 4 * q + 4, :].bitcast(I32))
-
         cw_sb = keep.tile([P, JB, PACK], F32, name="cw_sb")
         cb_sb = keep.tile([P, JB, PACK], F32, name="cb_sb")
         nc.sync.dma_start(cw_sb[:], cw.rearrange("(b p t) -> p b t", b=JB, t=PACK))
         nc.sync.dma_start(cb_sb[:], cb.rearrange("(b p t) -> p b t", b=JB, t=PACK))
+        tab_s = keep.tile([P, T // 4], I32, name="tab_s", align_bytes=64)
+        nc.vector.memset(tab_s[:], 0)
+        for q in range(4):
+            nc.sync.dma_start(tab_s[32 * q : 32 * q + 4, :], tab_scales[0, 4 * q : 4 * q + 4, :].bitcast(I32))
+
         al_s = keep.tile([P, N // 4], I32, name="al_s", align_bytes=64)
         nc.gpsimd.memset(al_s[:], 0)
-        for q in range(4):
-            nc.gpsimd.dma_start(al_s[32 * q : 32 * q + 16, :], al_scales[:, 4 * q : 4 * q + 4, :].bitcast(I32))
 
         x_raw = []
         for h in range(HALVES):
@@ -62,6 +60,8 @@ def tile_list_kernl_arc_none_kernel(
         nc.sync.dma_start(x_raw[1][:], x_rows[:, :, HALF:M])
         al_w = keep.tile([P, JB, N], I32, name="al_w", align_bytes=64)
         nc.sync.dma_start(al_w[:], al_words.rearrange("a p n i -> p a (n i)").bitcast(I32))
+        for q in range(4):
+            nc.sync.dma_start(al_s[32 * q : 32 * q + 16, :], al_scales[:, 4 * q : 4 * q + 4, :].bitcast(I32))
 
         sign = keep.tile([P, JB, PACK], F32, name="sign")
         mag = keep.tile([P, JB, PACK], F32, name="mag")

@@ -21,6 +21,7 @@ PASS = P * PACK
 JB = J // PASS
 HALF = 512
 HALVES = M // HALF
+QUARTER = 256
 NT = N // P
 
 
@@ -30,9 +31,9 @@ def tile_list_kernl_arc_none_kernel(
     nc = tc.nc
     with ExitStack() as ctx:
         keep = ctx.enter_context(tc.tile_pool(name="keep", bufs=1))
-        ring = ctx.enter_context(tc.tile_pool(name="ring", bufs=3))
+        ring = ctx.enter_context(tc.tile_pool(name="ring", bufs=4))
         xring = ctx.enter_context(tc.tile_pool(name="xring", bufs=2))
-        dpsum = ctx.enter_context(tc.psum_pool(name="dpsum", bufs=6))
+        dpsum = ctx.enter_context(tc.psum_pool(name="dpsum", bufs=4))
         ypsum = ctx.enter_context(tc.psum_pool(name="ypsum", bufs=1))
 
         offsets = keep.tile([P, J // 16], U16, name="offsets")
@@ -41,7 +42,12 @@ def tile_list_kernl_arc_none_kernel(
         cw_sb = keep.tile([P, JB, PACK], F32, name="cw_sb")
         cb_sb = keep.tile([P, JB, PACK], F32, name="cb_sb")
         nc.sync.dma_start(cw_sb[:], cw.rearrange("(b p t) -> p b t", b=JB, t=PACK))
-        nc.sync.dma_start(cb_sb[:], cb.rearrange("(b p t) -> p b t", b=JB, t=PACK))
+        x_raw = []
+        for h in range(HALVES):
+            x_raw.append(xring.tile([P, PACK, HALF], F32, name="x_raw"))
+        x_rows = x.rearrange("(p t) m -> p t m", t=PACK)
+        nc.sync.dma_start(x_raw[0][:, 0, :], x_rows[:, 0, 0:HALF])
+
         tab_s = keep.tile([P, T // 4], I32, name="tab_s", align_bytes=64)
         nc.vector.memset(tab_s[:], 0)
         for q in range(4):
@@ -50,13 +56,10 @@ def tile_list_kernl_arc_none_kernel(
         al_s = keep.tile([P, N // 4], I32, name="al_s", align_bytes=64)
         nc.gpsimd.memset(al_s[:], 0)
 
-        x_raw = []
-        for h in range(HALVES):
-            x_raw.append(xring.tile([P, PACK, HALF], F32, name="x_raw"))
-        x_rows = x.rearrange("(p t) m -> p t m", t=PACK)
-        nc.sync.dma_start(x_raw[0][:], x_rows[:, :, 0:HALF])
+        nc.sync.dma_start(x_raw[0][:, 1:PACK, :], x_rows[:, 1:PACK, 0:HALF])
         tab_w = keep.tile([P, T], I32, name="tab_w", align_bytes=64)
         nc.sync.dma_start(tab_w[:], tab_words[0].rearrange("p t i -> p (t i)").bitcast(I32))
+        nc.sync.dma_start(cb_sb[:], cb.rearrange("(b p t) -> p b t", b=JB, t=PACK))
         nc.sync.dma_start(x_raw[1][:], x_rows[:, :, HALF:M])
         al_w = keep.tile([P, JB, N], I32, name="al_w", align_bytes=64)
         nc.sync.dma_start(al_w[:], al_words.rearrange("a p n i -> p a (n i)").bitcast(I32))
@@ -66,9 +69,10 @@ def tile_list_kernl_arc_none_kernel(
         sign = keep.tile([P, JB, PACK], F32, name="sign")
         mag = keep.tile([P, JB, PACK], F32, name="mag")
         bias = keep.tile([P, JB, PACK], F32, name="bias")
-        nc.gpsimd.tensor_scalar(mag[:], cw_sb[:], 0.0, 2.0, ALU.is_ge, ALU.mult)
-        nc.gpsimd.tensor_scalar(sign[:], mag[:], 1.0, -1.0, ALU.mult, ALU.add)
-        nc.gpsimd.tensor_tensor(mag[:], cw_sb[:], sign[:], ALU.mult)
+        twice = keep.tile([P, JB, PACK], F32, name="twice")
+        nc.gpsimd.tensor_scalar(twice[:], cw_sb[:], 0.0, 2.0, ALU.is_ge, ALU.mult)
+        nc.gpsimd.tensor_scalar(sign[:], twice[:], 1.0, -1.0, ALU.mult, ALU.add)
+        nc.scalar.activation(mag[:], cw_sb[:], ACT.Abs)
         nc.gpsimd.tensor_tensor(bias[:], mag[:], cb_sb[:], ALU.mult)
 
         v_s = keep.tile([P, JB, PACK, P], U8, name="v_s", align_bytes=64)
@@ -86,10 +90,9 @@ def tile_list_kernl_arc_none_kernel(
         for b0, picked_s in picked:
             nc.vector.tensor_copy(v_s[:, b0 : b0 + 2], picked_s[:].rearrange("p (b c t) -> p b t c", b=2, t=PACK))
         x_s = keep.tile([P, M], U8, name="x_s", tag="early_a", align_bytes=64)
-        v_w = keep.tile([P, JB, PACK, P], U32, name="v_w", tag="early_b", align_bytes=64)
 
         def round_x(h):
-            x_bf = xring.tile([P, HALF, PACK], BF16, name="x_bf", align_bytes=64)
+            x_bf = keep.tile([P, HALF, PACK], BF16, name="x_bf", tag="early_c", align_bytes=64)
             nc.scalar.copy(
                 x_bf[:].rearrange("p (c i) t -> p c t i", i=4),
                 x_raw[h][:].rearrange("p t (c i) -> p c t i", i=4),
@@ -103,7 +106,17 @@ def tile_list_kernl_arc_none_kernel(
             )
 
         quantise_x(0, round_x(0))
-        x_next = round_x(1)
+        v_w = keep.tile([P, JB, PACK, P], U32, name="v_w", tag="early_c", align_bytes=64)
+        x_next = xring.tile([P, HALF, PACK], BF16, name="x_bf", align_bytes=64)
+        for c0 in range(0, HALF, QUARTER):
+            nc.gpsimd.tensor_scalar(
+                x_next[:, c0 : c0 + QUARTER, :],
+                x_raw[1][:, :, c0 : c0 + QUARTER].rearrange("p t m -> p m t"),
+                1.0,
+                0.0,
+                ALU.mult,
+                ALU.add,
+            )
 
         for b in range(JB):
             nc.vector.tensor_copy(
@@ -111,13 +124,11 @@ def tile_list_kernl_arc_none_kernel(
                 tab_w[:].bitcast(U32).indirect(offsets[:, b * cols_per_pass : (b + 1) * cols_per_pass]),
             )
 
-        quantise_x(1, x_next)
-
-        def first_product(h, b):
-            cols = slice(h * HALF, (h + 1) * HALF)
-            h_rows = ring.tile([P, PACK, HALF], BF16, name="h_rows", align_bytes=64)
+        def first_product(b, m0, width):
+            cols = slice(m0, m0 + width)
+            h_rows = ring.tile([P, PACK, width], BF16, name="h_rows", align_bytes=64)
             for t in range(PACK):
-                d = dpsum.tile([P, HALF], F32, name="d")
+                d = dpsum.tile([P, width], F32, name="d")
                 nc.tensor.matmul_mx(
                     out=d[:],
                     lhsT=v_w[:, b, t, :].bitcast(FP8X4),
@@ -136,8 +147,8 @@ def tile_list_kernl_arc_none_kernel(
             for t in range(PACK):
                 nc.vector.tensor_scalar(h_rows[:, t, :], h_rows[:, t, :], sign[:, b, t : t + 1], None, ALU.mult)
 
-        def interleave(h_rows):
-            h_bf = ring.tile([P, HALF, PACK], BF16, name="h_bf", align_bytes=64)
+        def interleave(h_rows, width):
+            h_bf = ring.tile([P, width, PACK], BF16, name="h_bf", align_bytes=64)
             nc.vector.tensor_copy(
                 h_bf[:].rearrange("p (c i) t -> p c t i", i=4),
                 h_rows[:].rearrange("p t (c i) -> p c t i", i=4),
@@ -145,39 +156,48 @@ def tile_list_kernl_arc_none_kernel(
             return h_bf
 
         y_acc = {}
+        y_banks = {0: ("y0", "y1"), HALF: ("y2", "y3"), HALF + QUARTER: ("y0", "y1")}
 
-        def second_product(h, b, h_bf):
-            h_w = ring.tile([P, HALF], U32, name="h_w", align_bytes=64)
-            h_s = ring.tile([P, HALF], U8, name="h_s", align_bytes=64)
+        def second_product(b, m0, width, h_bf):
+            h_w = ring.tile([P, width], U32, name="h_w", align_bytes=64)
+            h_s = ring.tile([P, width], U8, name="h_s", align_bytes=64)
             nc.vector.quantize_mx(out=h_w[:].bitcast(FP8X4), scales=h_s[:], in_=h_bf[:].rearrange("p m t -> p (m t)"))
-            for n in range(NT):
-                if b == 0:
-                    y_acc[n] = ypsum.tile([P, HALF], F32, name="y%d" % n)
-                rows = slice(n * P, (n + 1) * P)
-                nc.tensor.matmul_mx(
-                    out=y_acc[n][:],
-                    lhsT=al_w[:, b, rows].bitcast(FP8X4),
-                    lhsT_scale=al_s[:].bitcast(U8)[4 * b :, rows],
-                    rhs=h_w[:].bitcast(FP8X4),
-                    rhs_scale=h_s[:],
-                    start=(b == 0),
-                    stop=(b == JB - 1),
-                )
+            y_width = HALF if m0 < HALF else QUARTER
+            for c0 in range(0, width, y_width):
+                for n in range(NT):
+                    if b == 0:
+                        y_acc[n, m0 + c0] = ypsum.tile([P, y_width], F32, name="y", tag=y_banks[m0 + c0][n])
+                    rows = slice(n * P, (n + 1) * P)
+                    nc.tensor.matmul_mx(
+                        out=y_acc[n, m0 + c0][:],
+                        lhsT=al_w[:, b, rows].bitcast(FP8X4),
+                        lhsT_scale=al_s[:].bitcast(U8)[4 * b :, rows],
+                        rhs=h_w[:, c0 : c0 + y_width].bitcast(FP8X4),
+                        rhs_scale=h_s[:, c0 : c0 + y_width],
+                        start=(b == 0),
+                        stop=(b == JB - 1),
+                    )
             if b == JB - 1:
                 for n in range(NT):
-                    y_sb = xring.tile([P, HALF], F32, name="y_sb%d" % n)
-                    if h == HALVES - 1 and n == NT - 1:
-                        nc.vector.tensor_copy(y_sb[:], y_acc[n][:])
+                    y_sb = ring.tile([P, width], F32, name="y_sb%d" % n)
+                    if m0 + width == M and n == NT - 1:
+                        nc.vector.tensor_copy(y_sb[:], y_acc[n, m0][:])
                     else:
-                        nc.scalar.copy(y_sb[:], y_acc[n][:])
-                    nc.sync.dma_start(out[n * P : (n + 1) * P, h * HALF : (h + 1) * HALF], y_sb[:])
+                        nc.scalar.copy(y_sb[:], y_acc[n, m0][:])
+                    nc.sync.dma_start(out[n * P : (n + 1) * P, m0 : m0 + width], y_sb[:])
 
-        pending = None
-        for h in range(HALVES):
-            for b in range(JB):
-                h_rows = first_product(h, b)
-                apply_sign(b, h_rows)
-                if pending is not None:
-                    second_product(*pending)
-                pending = (h, b, interleave(h_rows))
-        second_product(*pending)
+        steps = [(b, m0, HALF) for m0 in range(0, M, HALF) for b in range(JB)][:-1]
+        steps.extend([(JB - 1, m0, QUARTER) for m0 in range(HALF, M, QUARTER)])
+        rows_of = {}
+        words_of = {}
+        for i in range(len(steps) + 2):
+            if i < len(steps):
+                rows_of[i] = first_product(*steps[i])
+            if 0 <= i - 1 < len(steps):
+                apply_sign(steps[i - 1][0], rows_of[i - 1])
+            if i == 2:
+                quantise_x(1, x_next)
+            if 0 <= i - 2:
+                second_product(*steps[i - 2], words_of[i - 2])
+            if 0 <= i - 1 < len(steps):
+                words_of[i - 1] = interleave(rows_of[i - 1], steps[i - 1][2])

@@ -40,27 +40,27 @@ def tile_list_kernl_arc_none_kernel(
         nc.sync.dma_start(offsets[:], offs)
 
         cw_sb = keep.tile([P, JB, PACK], F32, name="cw_sb")
-        cb_sb = keep.tile([P, JB, PACK], F32, name="cb_sb")
+        cb_sb = keep.tile([P, JB, PACK], F32, name="cb_sb", tag="early_d", align_bytes=64)
         nc.sync.dma_start(cw_sb[:], cw.rearrange("(b p t) -> p b t", b=JB, t=PACK))
-        x_raw = []
-        for h in range(HALVES):
-            x_raw.append(xring.tile([P, PACK, HALF], F32, name="x_raw"))
+        x_first = keep.tile([P, PACK, HALF], F32, name="x_first")
+        x_late = [xring.tile([P, PACK, QUARTER], F32, name="x_late") for u in range(2)]
         x_rows = x.rearrange("(p t) m -> p t m", t=PACK)
-        nc.sync.dma_start(x_raw[0][:, 0, :], x_rows[:, 0, 0:HALF])
 
         tab_s = keep.tile([P, T // 4], I32, name="tab_s", align_bytes=64)
-        nc.vector.memset(tab_s[:], 0)
+        nc.gpsimd.memset(tab_s[:, 0 : T // 8], 0)
+        nc.vector.memset(tab_s[:, T // 8 : T // 4], 0)
         for q in range(4):
             nc.sync.dma_start(tab_s[32 * q : 32 * q + 4, :], tab_scales[0, 4 * q : 4 * q + 4, :].bitcast(I32))
 
         al_s = keep.tile([P, N // 4], I32, name="al_s", align_bytes=64)
         nc.gpsimd.memset(al_s[:], 0)
 
-        nc.sync.dma_start(x_raw[0][:, 1:PACK, :], x_rows[:, 1:PACK, 0:HALF])
+        nc.sync.dma_start(x_first[:], x_rows[:, :, 0:HALF])
         tab_w = keep.tile([P, T], I32, name="tab_w", align_bytes=64)
         nc.sync.dma_start(tab_w[:], tab_words[0].rearrange("p t i -> p (t i)").bitcast(I32))
         nc.sync.dma_start(cb_sb[:], cb.rearrange("(b p t) -> p b t", b=JB, t=PACK))
-        nc.sync.dma_start(x_raw[1][:], x_rows[:, :, HALF:M])
+        for u in range(2):
+            nc.sync.dma_start(x_late[u][:], x_rows[:, :, HALF + u * QUARTER : HALF + (u + 1) * QUARTER])
         al_w = keep.tile([P, JB, N], I32, name="al_w", align_bytes=64)
         nc.sync.dma_start(al_w[:], al_words.rearrange("a p n i -> p a (n i)").bitcast(I32))
         for q in range(4):
@@ -69,11 +69,6 @@ def tile_list_kernl_arc_none_kernel(
         sign = keep.tile([P, JB, PACK], F32, name="sign")
         mag = keep.tile([P, JB, PACK], F32, name="mag")
         bias = keep.tile([P, JB, PACK], F32, name="bias")
-        twice = keep.tile([P, JB, PACK], F32, name="twice")
-        nc.gpsimd.tensor_scalar(twice[:], cw_sb[:], 0.0, 2.0, ALU.is_ge, ALU.mult)
-        nc.gpsimd.tensor_scalar(sign[:], twice[:], 1.0, -1.0, ALU.mult, ALU.add)
-        nc.scalar.activation(mag[:], cw_sb[:], ACT.Abs)
-        nc.gpsimd.tensor_tensor(bias[:], mag[:], cb_sb[:], ALU.mult)
 
         v_s = keep.tile([P, JB, PACK, P], U8, name="v_s", align_bytes=64)
         x_w = keep.tile([P, M], U32, name="x_w", align_bytes=64)
@@ -93,9 +88,10 @@ def tile_list_kernl_arc_none_kernel(
 
         def round_x(h):
             x_bf = keep.tile([P, HALF, PACK], BF16, name="x_bf", tag="early_c", align_bytes=64)
-            nc.scalar.copy(
+            nc.scalar.activation(
                 x_bf[:].rearrange("p (c i) t -> p c t i", i=4),
-                x_raw[h][:].rearrange("p t (c i) -> p c t i", i=4),
+                x_first[:].rearrange("p t (c i) -> p c t i", i=4),
+                ACT.Copy,
             )
             return x_bf
 
@@ -106,23 +102,33 @@ def tile_list_kernl_arc_none_kernel(
             )
 
         quantise_x(0, round_x(0))
-        v_w = keep.tile([P, JB, PACK, P], U32, name="v_w", tag="early_c", align_bytes=64)
+        v_first = keep.tile([P, PACK, P], U32, name="v_first", tag="early_c", align_bytes=64)
+
+        def gather_words(b, dst):
+            nc.vector.tensor_copy(
+                dst.rearrange("p t c -> p c t"),
+                tab_w[:].bitcast(U32).indirect(offsets[:, b * cols_per_pass : (b + 1) * cols_per_pass]),
+            )
+
+        gather_words(0, v_first[:])
+        nc.scalar.activation(mag[:], cw_sb[:], ACT.Abs)
+        nc.scalar.activation(sign[:], cw_sb[:], ACT.Sign)
+        nc.vector.tensor_tensor(bias[:], mag[:], cb_sb[:], ALU.mult)
+        v_rest = keep.tile([P, JB - 1, PACK, P], U32, name="v_rest", tag="early_d", align_bytes=64)
+        v_w = [v_first[:]] + [v_rest[:, b] for b in range(JB - 1)]
         x_next = xring.tile([P, HALF, PACK], BF16, name="x_bf", align_bytes=64)
         for c0 in range(0, HALF, QUARTER):
             nc.gpsimd.tensor_scalar(
                 x_next[:, c0 : c0 + QUARTER, :],
-                x_raw[1][:, :, c0 : c0 + QUARTER].rearrange("p t m -> p m t"),
+                x_late[c0 // QUARTER][:].rearrange("p t m -> p m t"),
                 1.0,
                 0.0,
                 ALU.mult,
                 ALU.add,
             )
 
-        for b in range(JB):
-            nc.vector.tensor_copy(
-                v_w[:, b].rearrange("p t c -> p c t"),
-                tab_w[:].bitcast(U32).indirect(offsets[:, b * cols_per_pass : (b + 1) * cols_per_pass]),
-            )
+        for b in range(1, JB):
+            gather_words(b, v_w[b])
 
         def first_product(b, m0, width):
             cols = slice(m0, m0 + width)
@@ -131,7 +137,7 @@ def tile_list_kernl_arc_none_kernel(
                 d = dpsum.tile([P, width], F32, name="d")
                 nc.tensor.matmul_mx(
                     out=d[:],
-                    lhsT=v_w[:, b, t, :].bitcast(FP8X4),
+                    lhsT=v_w[b][:, t, :].bitcast(FP8X4),
                     lhsT_scale=v_s[:, b, t, :],
                     rhs=x_w[:, cols].bitcast(FP8X4),
                     rhs_scale=x_s[:, cols],

@@ -39,39 +39,44 @@ def tile_list_kernl_arc_none_kernel(
         offsets = keep.tile([P, J // 16], U16, name="offsets")
         nc.sync.dma_start(offsets[:], offs)
 
-        cw_sb = keep.tile([P, JB, PACK], F32, name="cw_sb")
-        cb_sb = keep.tile([P, JB, PACK], F32, name="cb_sb", tag="early_d", align_bytes=64)
-        nc.sync.dma_start(cw_sb[:], cw.rearrange("(b p t) -> p b t", b=JB, t=PACK))
-        x_first = keep.tile([P, PACK, HALF], F32, name="x_first")
-        x_late = [xring.tile([P, PACK, QUARTER], F32, name="x_late") for u in range(2)]
-        x_rows = x.rearrange("(p t) m -> p t m", t=PACK)
-
+        al_s = keep.tile([P, N // 4], I32, name="al_s", align_bytes=64)
+        nc.gpsimd.memset(al_s[:], 0)
         tab_s = keep.tile([P, T // 4], I32, name="tab_s", align_bytes=64)
         nc.gpsimd.memset(tab_s[:, 0 : T // 8], 0)
         nc.vector.memset(tab_s[:, T // 8 : T // 4], 0)
-        for q in range(4):
-            nc.sync.dma_start(tab_s[32 * q : 32 * q + 4, :], tab_scales[0, 4 * q : 4 * q + 4, :].bitcast(I32))
 
-        al_s = keep.tile([P, N // 4], I32, name="al_s", align_bytes=64)
-        nc.gpsimd.memset(al_s[:], 0)
+        def load_al_scales(q):
+            nc.sync.dma_start(al_s[32 * q : 32 * q + 16, :], al_scales[:, 4 * q : 4 * q + 4, :].bitcast(I32))
 
-        nc.sync.dma_start(x_first[:], x_rows[:, :, 0:HALF])
+        load_al_scales(0)
+        for r in range(4):
+            nc.sync.dma_start(tab_s[r:P:32, :], tab_scales[0, r:16:4, :].bitcast(I32))
+
+        x_rows = x.rearrange("(p t) m -> p t m", t=PACK)
+        x_raw = [keep.tile([P, PACK, QUARTER], F32, name="x_raw%d" % u, tag="raw%d" % u, align_bytes=64) for u in range(4)]
+
+        def load_x(u):
+            nc.sync.dma_start(x_raw[u][:], x_rows[:, :, u * QUARTER : (u + 1) * QUARTER])
+
+        load_x(0)
         tab_w = keep.tile([P, T], I32, name="tab_w", align_bytes=64)
         nc.sync.dma_start(tab_w[:], tab_words[0].rearrange("p t i -> p (t i)").bitcast(I32))
+        cw_sb = keep.tile([P, JB, PACK], F32, name="cw_sb", tag="early_w", align_bytes=64)
+        cb_sb = keep.tile([P, JB, PACK], F32, name="cb_sb")
+        nc.sync.dma_start(cw_sb[:], cw.rearrange("(b p t) -> p b t", b=JB, t=PACK))
         nc.sync.dma_start(cb_sb[:], cb.rearrange("(b p t) -> p b t", b=JB, t=PACK))
-        for u in range(2):
-            nc.sync.dma_start(x_late[u][:], x_rows[:, :, HALF + u * QUARTER : HALF + (u + 1) * QUARTER])
+        for u in range(1, 4):
+            load_x(u)
         al_w = keep.tile([P, JB, N], I32, name="al_w", align_bytes=64)
         nc.sync.dma_start(al_w[:], al_words.rearrange("a p n i -> p a (n i)").bitcast(I32))
-        for q in range(4):
-            nc.sync.dma_start(al_s[32 * q : 32 * q + 16, :], al_scales[:, 4 * q : 4 * q + 4, :].bitcast(I32))
+        for q in range(1, 4):
+            load_al_scales(q)
 
         sign = keep.tile([P, JB, PACK], F32, name="sign")
         mag = keep.tile([P, JB, PACK], F32, name="mag")
         bias = keep.tile([P, JB, PACK], F32, name="bias")
 
-        v_s = keep.tile([P, JB, PACK, P], U8, name="v_s", align_bytes=64)
-        x_w = keep.tile([P, M], U32, name="x_w", align_bytes=64)
+        x_w = keep.tile([P, M], U32, name="x_w", tag="x_words", align_bytes=64)
 
         cols_per_pass = PASS // 16
         picked = []
@@ -82,27 +87,19 @@ def tile_list_kernl_arc_none_kernel(
                 tab_s[:].bitcast(U8).indirect(offsets[:, b0 * cols_per_pass : (b0 + 2) * cols_per_pass]),
             )
             picked.append((b0, picked_s))
-        for b0, picked_s in picked:
-            nc.vector.tensor_copy(v_s[:, b0 : b0 + 2], picked_s[:].rearrange("p (b c t) -> p b t c", b=2, t=PACK))
-        x_s = keep.tile([P, M], U8, name="x_s", tag="early_a", align_bytes=64)
 
-        def round_x(h):
-            x_bf = keep.tile([P, HALF, PACK], BF16, name="x_bf", tag="early_c", align_bytes=64)
-            nc.scalar.activation(
-                x_bf[:].rearrange("p (c i) t -> p c t i", i=4),
-                x_first[:].rearrange("p t (c i) -> p c t i", i=4),
-                ACT.Copy,
-            )
-            return x_bf
+        def reorder_scales(dst, src):
+            nc.vector.tensor_copy(dst[:], src[:].rearrange("p (b c t) -> p b t c", b=2, t=PACK))
 
-        def quantise_x(h, x_bf):
-            cols = slice(h * HALF, (h + 1) * HALF)
+        s_early = keep.tile([P, 2, PACK, P], U8, name="s_early", align_bytes=64)
+        reorder_scales(s_early, picked[0][1])
+        x_s = keep.tile([P, M], U8, name="x_s", align_bytes=64)
+
+        def quantise_x(u, x_bf):
+            cols = slice(u * QUARTER, (u + 1) * QUARTER)
             nc.vector.quantize_mx(
                 out=x_w[:, cols].bitcast(FP8X4), scales=x_s[:, cols], in_=x_bf[:].rearrange("p m t -> p (m t)")
             )
-
-        quantise_x(0, round_x(0))
-        v_first = keep.tile([P, PACK, P], U32, name="v_first", tag="early_c", align_bytes=64)
 
         def gather_words(b, dst):
             nc.vector.tensor_copy(
@@ -110,100 +107,134 @@ def tile_list_kernl_arc_none_kernel(
                 tab_w[:].bitcast(U32).indirect(offsets[:, b * cols_per_pass : (b + 1) * cols_per_pass]),
             )
 
+        x_bf = [keep.tile([P, QUARTER, PACK], BF16, name="x_bf0", align_bytes=64)]
+        nc.scalar.activation(
+            x_bf[0][:].rearrange("p (c i) t -> p c t i", i=4),
+            x_raw[0][:].rearrange("p t (c i) -> p c t i", i=4),
+            ACT.Copy,
+        )
+        quantise_x(0, x_bf[0])
+        v_first = keep.tile([P, PACK, P], U32, name="v_first", align_bytes=64)
         gather_words(0, v_first[:])
         nc.scalar.activation(mag[:], cw_sb[:], ACT.Abs)
         nc.scalar.activation(sign[:], cw_sb[:], ACT.Sign)
-        nc.vector.tensor_tensor(bias[:], mag[:], cb_sb[:], ALU.mult)
-        v_rest = keep.tile([P, JB - 1, PACK, P], U32, name="v_rest", tag="early_d", align_bytes=64)
-        v_w = [v_first[:]] + [v_rest[:, b] for b in range(JB - 1)]
-        x_next = xring.tile([P, HALF, PACK], BF16, name="x_bf", align_bytes=64)
-        for c0 in range(0, HALF, QUARTER):
+        nc.gpsimd.tensor_tensor(bias[:], mag[:], cb_sb[:], ALU.mult)
+        s_late = keep.tile([P, 2, PACK, P], U8, name="s_late", tag="early_w", align_bytes=64)
+        v_s = [s_early[:, 0], s_early[:, 1], s_late[:, 0], s_late[:, 1]]
+        v_mid = keep.tile([P, 2, PACK, P], U32, name="v_mid", align_bytes=64)
+        for u in range(1, 4):
+            x_bf.append(keep.tile([P, QUARTER, PACK], BF16, name="x_bf%d" % u, align_bytes=64))
             nc.gpsimd.tensor_scalar(
-                x_next[:, c0 : c0 + QUARTER, :],
-                x_late[c0 // QUARTER][:].rearrange("p t m -> p m t"),
-                1.0,
-                0.0,
-                ALU.mult,
-                ALU.add,
+                x_bf[u][:], x_raw[u][:].rearrange("p t m -> p m t"), 1.0, 0.0, ALU.mult, ALU.add
             )
+        gather_words(1, v_mid[:, 0])
+        reorder_scales(s_late, picked[1][1])
+        gather_words(2, v_mid[:, 1])
+        quantise_x(1, x_bf[1])
+        v_last = keep.tile([P, PACK, P], U32, name="v_last", tag="raw1", align_bytes=64)
+        gather_words(3, v_last[:])
+        v_w = [v_first[:], v_mid[:, 0], v_mid[:, 1], v_last[:]]
 
-        for b in range(1, JB):
-            gather_words(b, v_w[b])
+        steps = [(b, m0, HALF) for m0 in range(0, M, HALF) for b in range(JB)][:-1]
+        steps.extend([(JB - 1, m0, QUARTER) for m0 in range(HALF, M, QUARTER)])
+        rows_of = {}
 
-        def first_product(b, m0, width):
-            cols = slice(m0, m0 + width)
-            h_rows = ring.tile([P, PACK, width], BF16, name="h_rows", align_bytes=64)
+        def first_product(i, c0, width):
+            b, m0, step_width = steps[i]
+            cols = slice(m0 + c0, m0 + c0 + width)
+            if c0 == 0:
+                rows_of[i] = ring.tile([P, PACK, step_width], BF16, name="h_rows", align_bytes=64)
             for t in range(PACK):
                 d = dpsum.tile([P, width], F32, name="d")
                 nc.tensor.matmul_mx(
                     out=d[:],
                     lhsT=v_w[b][:, t, :].bitcast(FP8X4),
-                    lhsT_scale=v_s[:, b, t, :],
+                    lhsT_scale=v_s[b][:, t, :],
                     rhs=x_w[:, cols].bitcast(FP8X4),
                     rhs_scale=x_s[:, cols],
                     start=True,
                     stop=True,
                 )
                 nc.scalar.activation(
-                    h_rows[:, t, :], d[:], ACT.Relu, bias=bias[:, b, t : t + 1], scale=mag[:, b, t : t + 1]
+                    rows_of[i][:, t, c0 : c0 + width],
+                    d[:],
+                    ACT.Relu,
+                    bias=bias[:, b, t : t + 1],
+                    scale=mag[:, b, t : t + 1],
                 )
-            return h_rows
 
-        def apply_sign(b, h_rows):
+        def apply_sign(i):
+            b = steps[i][0]
             for t in range(PACK):
-                nc.vector.tensor_scalar(h_rows[:, t, :], h_rows[:, t, :], sign[:, b, t : t + 1], None, ALU.mult)
+                row = rows_of[i][:, t, :]
+                nc.vector.tensor_scalar(row, row, sign[:, b, t : t + 1], None, ALU.mult)
 
-        def interleave(h_rows, width):
-            h_bf = ring.tile([P, width, PACK], BF16, name="h_bf", align_bytes=64)
-            nc.vector.tensor_copy(
+        def interleave(i):
+            h_bf = ring.tile([P, steps[i][2], PACK], BF16, name="h_bf", align_bytes=64)
+            move = nc.scalar.copy if i == len(steps) - 2 else nc.vector.tensor_copy
+            move(
                 h_bf[:].rearrange("p (c i) t -> p c t i", i=4),
-                h_rows[:].rearrange("p t (c i) -> p c t i", i=4),
+                rows_of[i][:].rearrange("p t (c i) -> p c t i", i=4),
             )
             return h_bf
 
-        y_acc = {}
-        y_banks = {0: ("y0", "y1"), HALF: ("y2", "y3"), HALF + QUARTER: ("y0", "y1")}
+        y_half = [ypsum.tile([P, HALF], F32, name="y_half%d" % n) for n in range(NT)]
+        y_quarter = [ypsum.tile([P, NT, QUARTER], F32, name="y_quarter%d" % u) for u in range(2)]
 
-        def second_product(b, m0, width, h_bf):
+        def second_product(i, h_bf):
+            b, m0, width = steps[i]
             h_w = ring.tile([P, width], U32, name="h_w", align_bytes=64)
             h_s = ring.tile([P, width], U8, name="h_s", align_bytes=64)
             nc.vector.quantize_mx(out=h_w[:].bitcast(FP8X4), scales=h_s[:], in_=h_bf[:].rearrange("p m t -> p (m t)"))
             y_width = HALF if m0 < HALF else QUARTER
             for c0 in range(0, width, y_width):
                 for n in range(NT):
-                    if b == 0:
-                        y_acc[n, m0 + c0] = ypsum.tile([P, y_width], F32, name="y", tag=y_banks[m0 + c0][n])
                     rows = slice(n * P, (n + 1) * P)
+                    if m0 < HALF:
+                        acc, opens, closes = y_half[n][:], b == 0, b == JB - 1
+                    else:
+                        acc = y_quarter[(m0 + c0 - HALF) // QUARTER][:, n, :]
+                        opens, closes = b == 0 and n == 0, b == JB - 1 and n == NT - 1
                     nc.tensor.matmul_mx(
-                        out=y_acc[n, m0 + c0][:],
+                        out=acc,
                         lhsT=al_w[:, b, rows].bitcast(FP8X4),
                         lhsT_scale=al_s[:].bitcast(U8)[4 * b :, rows],
                         rhs=h_w[:, c0 : c0 + y_width].bitcast(FP8X4),
                         rhs_scale=h_s[:, c0 : c0 + y_width],
-                        start=(b == 0),
-                        stop=(b == JB - 1),
+                        start=opens,
+                        stop=closes,
                     )
-            if b == JB - 1:
-                for n in range(NT):
-                    y_sb = ring.tile([P, width], F32, name="y_sb%d" % n)
-                    if m0 + width == M and n == NT - 1:
-                        nc.vector.tensor_copy(y_sb[:], y_acc[n, m0][:])
-                    else:
-                        nc.scalar.copy(y_sb[:], y_acc[n, m0][:])
-                    nc.sync.dma_start(out[n * P : (n + 1) * P, m0 : m0 + width], y_sb[:])
 
-        steps = [(b, m0, HALF) for m0 in range(0, M, HALF) for b in range(JB)][:-1]
-        steps.extend([(JB - 1, m0, QUARTER) for m0 in range(HALF, M, QUARTER)])
-        rows_of = {}
+        def store_half(n):
+            y_sb = keep.tile([P, HALF], F32, name="y_sb%d" % n, tag=("x_words", "raw1")[n], align_bytes=64)
+            nc.scalar.copy(y_sb[:], y_half[n][:])
+            nc.sync.dma_start(out[n * P : (n + 1) * P, 0:HALF], y_sb[:])
+
+        def store_quarter(u):
+            y_sb = keep.tile([P, NT, QUARTER], F32, name="y_sbq%d" % u)
+            (nc.scalar.copy, nc.vector.tensor_copy)[u](y_sb[:], y_quarter[u][:])
+            m0 = HALF + u * QUARTER
+            nc.sync.dma_start(out[:, m0 : m0 + QUARTER].rearrange("(n p) m -> p n m", n=NT), y_sb[:])
+
+        for c0 in (0, QUARTER):
+            first_product(0, c0, QUARTER)
+            first_product(1, c0, QUARTER)
         words_of = {}
-        for i in range(len(steps) + 2):
-            if i < len(steps):
-                rows_of[i] = first_product(*steps[i])
-            if 0 <= i - 1 < len(steps):
-                apply_sign(steps[i - 1][0], rows_of[i - 1])
-            if i == 2:
-                quantise_x(1, x_next)
+        last = len(steps) - 1
+        for i in range(1, last + 3):
+            if 2 <= i <= last:
+                first_product(i, 0, steps[i][2])
+            if i == last:
+                store_half(0)
+            if i - 1 <= last:
+                apply_sign(i - 1)
+            if i in (1, 2):
+                quantise_x(i + 1, x_bf[i + 1])
             if 0 <= i - 2:
-                second_product(*steps[i - 2], words_of[i - 2])
-            if 0 <= i - 1 < len(steps):
-                words_of[i - 1] = interleave(rows_of[i - 1], steps[i - 1][2])
+                second_product(i - 2, words_of[i - 2])
+            if i - 1 <= last:
+                words_of[i - 1] = interleave(i - 1)
+            if i == last:
+                store_half(1)
+            if i - 2 >= last - 1:
+                store_quarter(i - 2 - (last - 1))

@@ -53,20 +53,16 @@ def tile_list_kernl_arc_none_kernel(
             nc.sync.dma_start(tab_s[r:P:32, :], tab_scales[0, r:16:4, :].bitcast(I32))
 
         x_rows = x.rearrange("(p t) m -> p t m", t=PACK)
-        x_raw = [keep.tile([P, PACK, QUARTER], F32, name="x_raw%d" % u, tag="raw%d" % u, align_bytes=64) for u in range(4)]
-
-        def load_x(u):
-            nc.sync.dma_start(x_raw[u][:], x_rows[:, :, u * QUARTER : (u + 1) * QUARTER])
-
-        load_x(0)
+        x_first = keep.tile([P, PACK, HALF], F32, name="x_first")
+        nc.sync.dma_start(x_first[:], x_rows[:, :, 0:HALF])
         tab_w = keep.tile([P, T], I32, name="tab_w", align_bytes=64)
         nc.sync.dma_start(tab_w[:], tab_words[0].rearrange("p t i -> p (t i)").bitcast(I32))
         cw_sb = keep.tile([P, JB, PACK], F32, name="cw_sb", tag="early_w", align_bytes=64)
         cb_sb = keep.tile([P, JB, PACK], F32, name="cb_sb")
-        nc.sync.dma_start(cw_sb[:], cw.rearrange("(b p t) -> p b t", b=JB, t=PACK))
         nc.sync.dma_start(cb_sb[:], cb.rearrange("(b p t) -> p b t", b=JB, t=PACK))
-        for u in range(1, 4):
-            load_x(u)
+        nc.sync.dma_start(cw_sb[:], cw.rearrange("(b p t) -> p b t", b=JB, t=PACK))
+        x_late = keep.tile([P, PACK, HALF], F32, name="x_late")
+        nc.sync.dma_start(x_late[:], x_rows[:, :, HALF:M])
         al_w = keep.tile([P, JB, N], I32, name="al_w", align_bytes=64)
         nc.sync.dma_start(al_w[:], al_words.rearrange("a p n i -> p a (n i)").bitcast(I32))
         for q in range(1, 4):
@@ -76,27 +72,27 @@ def tile_list_kernl_arc_none_kernel(
         mag = keep.tile([P, JB, PACK], F32, name="mag")
         bias = keep.tile([P, JB, PACK], F32, name="bias")
 
+        v_s = keep.tile([P, JB, PACK, P], U8, name="v_s", align_bytes=64)
         x_w = keep.tile([P, M], U32, name="x_w", tag="x_words", align_bytes=64)
+        x_s = keep.tile([P, M], U8, name="x_s", align_bytes=64)
 
         cols_per_pass = PASS // 16
         picked = []
-        for b0, shared in ((0, "early_a"), (2, "early_b")):
-            picked_s = keep.tile([P, 2 * PASS], U8, name="picked_s", tag=shared, align_bytes=64)
+        for b0 in (0, 2):
+            picked_s = keep.tile([P, 2 * PASS], U8, name="picked_s%d" % b0, align_bytes=64)
             nc.vector.tensor_copy(
                 picked_s[:],
                 tab_s[:].bitcast(U8).indirect(offsets[:, b0 * cols_per_pass : (b0 + 2) * cols_per_pass]),
             )
             picked.append((b0, picked_s))
+        for b0, picked_s in picked:
+            nc.vector.tensor_copy(v_s[:, b0 : b0 + 2], picked_s[:].rearrange("p (b c t) -> p b t c", b=2, t=PACK))
 
-        def reorder_scales(dst, src):
-            nc.vector.tensor_copy(dst[:], src[:].rearrange("p (b c t) -> p b t c", b=2, t=PACK))
+        def by_fours(dst, src):
+            return dst.rearrange("p (c i) t -> p c t i", i=4), src.rearrange("p t (c i) -> p c t i", i=4)
 
-        s_early = keep.tile([P, 2, PACK, P], U8, name="s_early", align_bytes=64)
-        reorder_scales(s_early, picked[0][1])
-        x_s = keep.tile([P, M], U8, name="x_s", align_bytes=64)
-
-        def quantise_x(u, x_bf):
-            cols = slice(u * QUARTER, (u + 1) * QUARTER)
+        def quantise_x(h, x_bf):
+            cols = slice(h * HALF, (h + 1) * HALF)
             nc.vector.quantize_mx(
                 out=x_w[:, cols].bitcast(FP8X4), scales=x_s[:, cols], in_=x_bf[:].rearrange("p m t -> p (m t)")
             )
@@ -107,33 +103,19 @@ def tile_list_kernl_arc_none_kernel(
                 tab_w[:].bitcast(U32).indirect(offsets[:, b * cols_per_pass : (b + 1) * cols_per_pass]),
             )
 
-        x_bf = [keep.tile([P, QUARTER, PACK], BF16, name="x_bf0", align_bytes=64)]
-        nc.scalar.activation(
-            x_bf[0][:].rearrange("p (c i) t -> p c t i", i=4),
-            x_raw[0][:].rearrange("p t (c i) -> p c t i", i=4),
-            ACT.Copy,
-        )
+        x_bf = [keep.tile([P, HALF, PACK], BF16, name="x_bf%d" % h, align_bytes=64) for h in range(HALVES)]
+        nc.scalar.activation(*by_fours(x_bf[0][:], x_first[:]), ACT.Copy)
         quantise_x(0, x_bf[0])
         v_first = keep.tile([P, PACK, P], U32, name="v_first", align_bytes=64)
         gather_words(0, v_first[:])
         nc.scalar.activation(mag[:], cw_sb[:], ACT.Abs)
         nc.scalar.activation(sign[:], cw_sb[:], ACT.Sign)
-        nc.gpsimd.tensor_tensor(bias[:], mag[:], cb_sb[:], ALU.mult)
-        s_late = keep.tile([P, 2, PACK, P], U8, name="s_late", tag="early_w", align_bytes=64)
-        v_s = [s_early[:, 0], s_early[:, 1], s_late[:, 0], s_late[:, 1]]
-        v_mid = keep.tile([P, 2, PACK, P], U32, name="v_mid", align_bytes=64)
-        for u in range(1, 4):
-            x_bf.append(keep.tile([P, QUARTER, PACK], BF16, name="x_bf%d" % u, align_bytes=64))
-            nc.gpsimd.tensor_scalar(
-                x_bf[u][:], x_raw[u][:].rearrange("p t m -> p m t"), 1.0, 0.0, ALU.mult, ALU.add
-            )
-        gather_words(1, v_mid[:, 0])
-        reorder_scales(s_late, picked[1][1])
-        gather_words(2, v_mid[:, 1])
-        quantise_x(1, x_bf[1])
-        v_last = keep.tile([P, PACK, P], U32, name="v_last", tag="raw1", align_bytes=64)
-        gather_words(3, v_last[:])
-        v_w = [v_first[:], v_mid[:, 0], v_mid[:, 1], v_last[:]]
+        nc.vector.tensor_tensor(bias[:], mag[:], cb_sb[:], ALU.mult)
+        v_rest = keep.tile([P, JB - 1, PACK, P], U32, name="v_rest", tag="early_w", align_bytes=64)
+        for b in range(1, JB):
+            gather_words(b, v_rest[:, b - 1])
+        v_w = [v_first[:]] + [v_rest[:, b] for b in range(JB - 1)]
+        nc.vector.tensor_copy(*by_fours(x_bf[1][:], x_late[:]))
 
         steps = [(b, m0, HALF) for m0 in range(0, M, HALF) for b in range(JB)][:-1]
         steps.extend([(JB - 1, m0, QUARTER) for m0 in range(HALF, M, QUARTER)])
@@ -149,7 +131,7 @@ def tile_list_kernl_arc_none_kernel(
                 nc.tensor.matmul_mx(
                     out=d[:],
                     lhsT=v_w[b][:, t, :].bitcast(FP8X4),
-                    lhsT_scale=v_s[b][:, t, :],
+                    lhsT_scale=v_s[:, b, t, :],
                     rhs=x_w[:, cols].bitcast(FP8X4),
                     rhs_scale=x_s[:, cols],
                     start=True,
@@ -206,7 +188,7 @@ def tile_list_kernl_arc_none_kernel(
                     )
 
         def store_half(n):
-            y_sb = keep.tile([P, HALF], F32, name="y_sb%d" % n, tag=("x_words", "raw1")[n], align_bytes=64)
+            y_sb = keep.tile([P, HALF], F32, name="y_sb%d" % n, tag=("x_words", "early_w")[n], align_bytes=64)
             nc.scalar.copy(y_sb[:], y_half[n][:])
             nc.sync.dma_start(out[n * P : (n + 1) * P, 0:HALF], y_sb[:])
 
@@ -216,20 +198,18 @@ def tile_list_kernl_arc_none_kernel(
             m0 = HALF + u * QUARTER
             nc.sync.dma_start(out[:, m0 : m0 + QUARTER].rearrange("(n p) m -> p n m", n=NT), y_sb[:])
 
-        for c0 in (0, QUARTER):
-            first_product(0, c0, QUARTER)
-            first_product(1, c0, QUARTER)
+        first_product(0, 0, HALF)
         words_of = {}
         last = len(steps) - 1
         for i in range(1, last + 3):
-            if 2 <= i <= last:
+            if i <= last:
                 first_product(i, 0, steps[i][2])
             if i == last:
                 store_half(0)
             if i - 1 <= last:
                 apply_sign(i - 1)
-            if i in (1, 2):
-                quantise_x(i + 1, x_bf[i + 1])
+            if i == 2:
+                quantise_x(1, x_bf[1])
             if 0 <= i - 2:
                 second_product(i - 2, words_of[i - 2])
             if i - 1 <= last:

@@ -48,12 +48,12 @@ def tile_list_kernl_arc_none_kernel(
         def load_al_scales(q):
             nc.sync.dma_start(al_s[32 * q : 32 * q + 16, :], al_scales[:, 4 * q : 4 * q + 4, :].bitcast(I32))
 
-        load_al_scales(0)
-        for r in range(4):
-            nc.sync.dma_start(tab_s[r:P:32, :], tab_scales[0, r:16:4, :].bitcast(I32))
+        for q in range(4):
+            load_al_scales(q)
+        nc.sync.dma_start(tab_s[0:P:8, :], tab_scales[0].bitcast(I32))
 
         x_rows = x.rearrange("(p t) m -> p t m", t=PACK)
-        x_first = keep.tile([P, PACK, HALF], F32, name="x_first")
+        x_first = keep.tile([P, PACK, HALF], F32, name="x_first", tag="early_x", align_bytes=64)
         nc.sync.dma_start(x_first[:], x_rows[:, :, 0:HALF])
         tab_w = keep.tile([P, T], I32, name="tab_w", align_bytes=64)
         nc.sync.dma_start(tab_w[:], tab_words[0].rearrange("p t i -> p (t i)").bitcast(I32))
@@ -65,14 +65,11 @@ def tile_list_kernl_arc_none_kernel(
         nc.sync.dma_start(x_late[:], x_rows[:, :, HALF:M])
         al_w = keep.tile([P, JB, N], I32, name="al_w", align_bytes=64)
         nc.sync.dma_start(al_w[:], al_words.rearrange("a p n i -> p a (n i)").bitcast(I32))
-        for q in range(1, 4):
-            load_al_scales(q)
 
         sign = keep.tile([P, JB, PACK], F32, name="sign")
         mag = keep.tile([P, JB, PACK], F32, name="mag")
         bias = keep.tile([P, JB, PACK], F32, name="bias")
 
-        v_s = keep.tile([P, JB, PACK, P], U8, name="v_s", align_bytes=64)
         x_w = keep.tile([P, M], U32, name="x_w", tag="x_words", align_bytes=64)
         x_s = keep.tile([P, M], U8, name="x_s", align_bytes=64)
 
@@ -85,8 +82,6 @@ def tile_list_kernl_arc_none_kernel(
                 tab_s[:].bitcast(U8).indirect(offsets[:, b0 * cols_per_pass : (b0 + 2) * cols_per_pass]),
             )
             picked.append((b0, picked_s))
-        for b0, picked_s in picked:
-            nc.vector.tensor_copy(v_s[:, b0 : b0 + 2], picked_s[:].rearrange("p (b c t) -> p b t c", b=2, t=PACK))
 
         def by_fours(dst, src):
             return dst.rearrange("p (c i) t -> p c t i", i=4), src.rearrange("p t (c i) -> p c t i", i=4)
@@ -105,6 +100,13 @@ def tile_list_kernl_arc_none_kernel(
 
         x_bf = [keep.tile([P, HALF, PACK], BF16, name="x_bf%d" % h, align_bytes=64) for h in range(HALVES)]
         nc.scalar.activation(*by_fours(x_bf[0][:], x_first[:]), ACT.Copy)
+        v_s = keep.tile([P, JB, PACK, P], U8, name="v_s", tag="early_x", align_bytes=64)
+        v_s_words = v_s[:].rearrange("p b t c -> p (b t c)").bitcast(I32)
+        for b0, picked_s in picked:
+            nc.vector.tensor_copy(v_s[:, b0 : b0 + 2], picked_s[:].rearrange("p (b c t) -> p b t c", b=2, t=PACK))
+            cols = slice(b0 * P, (b0 + 2) * P)
+            for r in range(1, 4):
+                nc.scalar.dma_start(v_s_words[r:P:32, cols], v_s_words[8 * r : P : 32, cols])
         quantise_x(0, x_bf[0])
         v_first = keep.tile([P, PACK, P], U32, name="v_first", align_bytes=64)
         gather_words(0, v_first[:])

@@ -23,6 +23,7 @@ HALF = 512
 HALVES = M // HALF
 QUARTER = 256
 NT = N // P
+SHARE = 128
 
 
 def tile_list_kernl_arc_none_kernel(
@@ -45,6 +46,10 @@ def tile_list_kernl_arc_none_kernel(
         nc.gpsimd.memset(tab_s[:, 0 : T // 8], 0)
         nc.vector.memset(tab_s[:, T // 8 : T // 4], 0)
 
+        v_s_words = keep.tile([P, J // 4], I32, name="v_s_words", align_bytes=64)
+        nc.gpsimd.memset(v_s_words[:], 0)
+        v_s = v_s_words[:].bitcast(U8).rearrange("p (b t c) -> p b t c", b=JB, t=PACK)
+
         def load_al_scales(q):
             nc.sync.dma_start(al_s[32 * q : 32 * q + 16, :], al_scales[:, 4 * q : 4 * q + 4, :].bitcast(I32))
 
@@ -53,7 +58,7 @@ def tile_list_kernl_arc_none_kernel(
         nc.sync.dma_start(tab_s[0:P:8, :], tab_scales[0].bitcast(I32))
 
         x_rows = x.rearrange("(p t) m -> p t m", t=PACK)
-        x_first = keep.tile([P, PACK, HALF], F32, name="x_first", tag="early_x", align_bytes=64)
+        x_first = keep.tile([P, PACK, HALF], F32, name="x_first")
         nc.sync.dma_start(x_first[:], x_rows[:, :, 0:HALF])
         tab_w = keep.tile([P, T], I32, name="tab_w", align_bytes=64)
         nc.sync.dma_start(tab_w[:], tab_words[0].rearrange("p t i -> p (t i)").bitcast(I32))
@@ -61,10 +66,6 @@ def tile_list_kernl_arc_none_kernel(
         cb_sb = keep.tile([P, JB, PACK], F32, name="cb_sb")
         nc.sync.dma_start(cb_sb[:], cb.rearrange("(b p t) -> p b t", b=JB, t=PACK))
         nc.sync.dma_start(cw_sb[:], cw.rearrange("(b p t) -> p b t", b=JB, t=PACK))
-        x_late = keep.tile([P, PACK, HALF], F32, name="x_late")
-        nc.sync.dma_start(x_late[:], x_rows[:, :, HALF:M])
-        al_w = keep.tile([P, JB, N], I32, name="al_w", align_bytes=64)
-        nc.sync.dma_start(al_w[:], al_words.rearrange("a p n i -> p a (n i)").bitcast(I32))
 
         sign = keep.tile([P, JB, PACK], F32, name="sign")
         mag = keep.tile([P, JB, PACK], F32, name="mag")
@@ -76,7 +77,7 @@ def tile_list_kernl_arc_none_kernel(
         cols_per_pass = PASS // 16
         picked = []
         for b0 in (0, 2):
-            picked_s = keep.tile([P, 2 * PASS], U8, name="picked_s%d" % b0, align_bytes=64)
+            picked_s = keep.tile([P, 2 * PASS], U8, name="picked_s", tag="picked%d" % b0, align_bytes=64)
             nc.vector.tensor_copy(
                 picked_s[:],
                 tab_s[:].bitcast(U8).indirect(offsets[:, b0 * cols_per_pass : (b0 + 2) * cols_per_pass]),
@@ -100,13 +101,22 @@ def tile_list_kernl_arc_none_kernel(
 
         x_bf = [keep.tile([P, HALF, PACK], BF16, name="x_bf%d" % h, align_bytes=64) for h in range(HALVES)]
         nc.scalar.activation(*by_fours(x_bf[0][:], x_first[:]), ACT.Copy)
-        v_s = keep.tile([P, JB, PACK, P], U8, name="v_s", tag="early_x", align_bytes=64)
-        v_s_words = v_s[:].rearrange("p b t c -> p (b t c)").bitcast(I32)
-        for b0, picked_s in picked:
-            nc.vector.tensor_copy(v_s[:, b0 : b0 + 2], picked_s[:].rearrange("p (b c t) -> p b t c", b=2, t=PACK))
-            cols = slice(b0 * P, (b0 + 2) * P)
-            for r in range(1, 4):
-                nc.scalar.dma_start(v_s_words[r:P:32, cols], v_s_words[8 * r : P : 32, cols])
+
+        def place_scales(b0, picked_s):
+            by_slot = keep.tile([P, 2 * P], I32, name="by_slot%d" % b0, align_bytes=64)
+            nc.vector.tensor_copy(
+                by_slot[:].bitcast(U8).rearrange("p (b t c) -> p b t c", b=2, t=PACK),
+                picked_s[:].rearrange("p (b c t) -> p b t c", b=2, t=PACK),
+            )
+            for r in range(4):
+                nc.sync.dma_start(v_s_words[r:P:32, b0 * P : (b0 + 2) * P], by_slot[8 * r : P : 32, :])
+
+        place_scales(*picked[0])
+        x_late = keep.tile([P, PACK, HALF], F32, name="x_late", tag="picked0", align_bytes=64)
+        nc.sync.dma_start(x_late[:], x_rows[:, :, HALF:M])
+        place_scales(*picked[1])
+        al_w = keep.tile([P, JB, N], I32, name="al_w", tag="picked2", align_bytes=64)
+        nc.sync.dma_start(al_w[:], al_words.rearrange("a p n i -> p a (n i)").bitcast(I32))
         quantise_x(0, x_bf[0])
         v_first = keep.tile([P, PACK, P], U32, name="v_first", align_bytes=64)
         gather_words(0, v_first[:])
@@ -117,7 +127,7 @@ def tile_list_kernl_arc_none_kernel(
         for b in range(1, JB):
             gather_words(b, v_rest[:, b - 1])
         v_w = [v_first[:]] + [v_rest[:, b] for b in range(JB - 1)]
-        nc.vector.tensor_copy(*by_fours(x_bf[1][:], x_late[:]))
+        nc.vector.tensor_copy(*by_fours(x_bf[1][:, SHARE:, :], x_late[:, :, SHARE:]))
 
         steps = [(b, m0, HALF) for m0 in range(0, M, HALF) for b in range(JB)][:-1]
         steps.extend([(JB - 1, m0, QUARTER) for m0 in range(HALF, M, QUARTER)])
@@ -201,6 +211,7 @@ def tile_list_kernl_arc_none_kernel(
             nc.sync.dma_start(out[:, m0 : m0 + QUARTER].rearrange("(n p) m -> p n m", n=NT), y_sb[:])
 
         first_product(0, 0, HALF)
+        nc.scalar.activation(*by_fours(x_bf[1][:, :SHARE, :], x_late[:, :, :SHARE]), ACT.Copy)
         words_of = {}
         last = len(steps) - 1
         for i in range(1, last + 3):

@@ -84,8 +84,8 @@ def tile_list_kernl_arc_none_kernel(
             )
             picked.append((b0, picked_s))
 
-        def by_fours(dst, src):
-            return dst.rearrange("p (c i) t -> p c t i", i=4), src.rearrange("p t (c i) -> p c t i", i=4)
+        def by_fours(dst, src, run=4):
+            return dst.rearrange("p (c i) t -> p c t i", i=run), src.rearrange("p t (c i) -> p c t i", i=run)
 
         def quantise_x(h, x_bf):
             cols = slice(h * HALF, (h + 1) * HALF)
@@ -129,8 +129,7 @@ def tile_list_kernl_arc_none_kernel(
         v_w = [v_first[:]] + [v_rest[:, b] for b in range(JB - 1)]
         nc.vector.tensor_copy(*by_fours(x_bf[1][:, SHARE:, :], x_late[:, :, SHARE:]))
 
-        steps = [(b, m0, HALF) for m0 in range(0, M, HALF) for b in range(JB)][:-1]
-        steps.extend([(JB - 1, m0, QUARTER) for m0 in range(HALF, M, QUARTER)])
+        steps = [(b, m0, HALF) for m0 in range(0, M, HALF) for b in range(JB)]
         rows_of = {}
 
         def first_product(i, c0, width):
@@ -163,20 +162,15 @@ def tile_list_kernl_arc_none_kernel(
                 row = rows_of[i][:, t, :]
                 nc.vector.tensor_scalar(row, row, sign[:, b, t : t + 1], None, ALU.mult)
 
-        def interleave(i):
-            h_bf = ring.tile([P, steps[i][2], PACK], BF16, name="h_bf", align_bytes=64)
-            move = nc.scalar.copy if i == len(steps) - 2 else nc.vector.tensor_copy
-            move(
-                h_bf[:].rearrange("p (c i) t -> p c t i", i=4),
-                rows_of[i][:].rearrange("p t (c i) -> p c t i", i=4),
-            )
+        def interleave(i, c0, width, move, run):
+            h_bf = ring.tile([P, width, PACK], BF16, name="h_bf", align_bytes=64)
+            move(*by_fours(h_bf[:], rows_of[i][:, :, c0 : c0 + width], run))
             return h_bf
 
         y_half = [ypsum.tile([P, HALF], F32, name="y_half%d" % n) for n in range(NT)]
         y_quarter = [ypsum.tile([P, NT, QUARTER], F32, name="y_quarter%d" % u) for u in range(2)]
 
-        def second_product(i, h_bf):
-            b, m0, width = steps[i]
+        def second_product(b, m0, width, h_bf):
             h_w = ring.tile([P, width], U32, name="h_w", align_bytes=64)
             h_s = ring.tile([P, width], U8, name="h_s", align_bytes=64)
             nc.vector.quantize_mx(out=h_w[:].bitcast(FP8X4), scales=h_s[:], in_=h_bf[:].rearrange("p m t -> p (m t)"))
@@ -214,20 +208,21 @@ def tile_list_kernl_arc_none_kernel(
         nc.scalar.activation(*by_fours(x_bf[1][:, :SHARE, :], x_late[:, :, :SHARE]), ACT.Copy)
         words_of = {}
         last = len(steps) - 1
-        for i in range(1, last + 3):
+        for i in range(1, last + 2):
             if i <= last:
-                first_product(i, 0, steps[i][2])
+                first_product(i, 0, HALF)
             if i == last:
                 store_half(0)
-            if i - 1 <= last:
-                apply_sign(i - 1)
+            apply_sign(i - 1)
             if i == 2:
                 quantise_x(1, x_bf[1])
             if 0 <= i - 2:
-                second_product(i - 2, words_of[i - 2])
-            if i - 1 <= last:
-                words_of[i - 1] = interleave(i - 1)
-            if i == last:
-                store_half(1)
-            if i - 2 >= last - 1:
-                store_quarter(i - 2 - (last - 1))
+                second_product(*steps[i - 2], words_of[i - 2])
+            if i - 1 < last:
+                words_of[i - 1] = interleave(i - 1, 0, HALF, nc.vector.tensor_copy, 8)
+        third = interleave(last, 0, QUARTER, nc.vector.tensor_copy, 8)
+        fourth = interleave(last, QUARTER, QUARTER, nc.scalar.copy, 4)
+        store_half(1)
+        for u, h_bf in enumerate((third, fourth)):
+            second_product(JB - 1, HALF + u * QUARTER, QUARTER, h_bf)
+            store_quarter(u)

@@ -24,6 +24,7 @@ HALVES = M // HALF
 QUARTER = 256
 NT = N // P
 SHARE = 128
+ROWS0 = P - 16
 
 
 def tile_list_kernl_arc_none_kernel(
@@ -43,8 +44,9 @@ def tile_list_kernl_arc_none_kernel(
         al_s = keep.tile([P, N // 4], I32, name="al_s", align_bytes=64)
         nc.gpsimd.memset(al_s[:], 0)
         tab_s = keep.tile([P, T // 4], I32, name="tab_s", align_bytes=64)
-        nc.gpsimd.memset(tab_s[:, 0 : T // 8], 0)
-        nc.vector.memset(tab_s[:, T // 8 : T // 4], 0)
+        nc.sync.dma_start(tab_s[ROWS0:P, :], tab_scales[0].bitcast(I32))
+        nc.gpsimd.memset(tab_s[0:ROWS0, 0 : T // 8], 0)
+        nc.vector.memset(tab_s[0:ROWS0, T // 8 : T // 4], 0)
 
         v_s_words = keep.tile([P, J // 4], I32, name="v_s_words", align_bytes=64)
         nc.gpsimd.memset(v_s_words[:], 0)
@@ -55,7 +57,6 @@ def tile_list_kernl_arc_none_kernel(
 
         for q in range(4):
             load_al_scales(q)
-        nc.sync.dma_start(tab_s[0:P:8, :], tab_scales[0].bitcast(I32))
 
         x_rows = x.rearrange("(p t) m -> p t m", t=PACK)
         x_first = keep.tile([P, PACK, HALF], F32, name="x_first")
@@ -108,8 +109,10 @@ def tile_list_kernl_arc_none_kernel(
                 by_slot[:].bitcast(U8).rearrange("p (b t c) -> p b t c", b=2, t=PACK),
                 picked_s[:].rearrange("p (b c t) -> p b t c", b=2, t=PACK),
             )
-            for r in range(4):
-                nc.sync.dma_start(v_s_words[r:P:32, b0 * P : (b0 + 2) * P], by_slot[8 * r : P : 32, :])
+            for q in range(4):
+                nc.sync.dma_start(
+                    v_s_words[32 * q : 32 * q + 4, b0 * P : (b0 + 2) * P], by_slot[ROWS0 + 4 * q : ROWS0 + 4 * q + 4, :]
+                )
 
         place_scales(*picked[0])
         x_late = keep.tile([P, PACK, HALF], F32, name="x_late", tag="picked0", align_bytes=64)

@@ -23,7 +23,7 @@ HALF = 512
 HALVES = M // HALF
 QUARTER = 256
 NT = N // P
-SHARE = 128
+SHARE = 256
 ROWS0 = P - 16
 
 
@@ -34,29 +34,20 @@ def tile_list_kernl_arc_none_kernel(
     with ExitStack() as ctx:
         keep = ctx.enter_context(tc.tile_pool(name="keep", bufs=1))
         ring = ctx.enter_context(tc.tile_pool(name="ring", bufs=4))
-        xring = ctx.enter_context(tc.tile_pool(name="xring", bufs=2))
+        reuse = ctx.enter_context(tc.tile_pool(name="reuse", bufs=1))
         dpsum = ctx.enter_context(tc.psum_pool(name="dpsum", bufs=4))
         ypsum = ctx.enter_context(tc.psum_pool(name="ypsum", bufs=1))
 
         offsets = keep.tile([P, J // 16], U16, name="offsets")
         nc.sync.dma_start(offsets[:], offs)
 
-        al_s = keep.tile([P, N // 4], I32, name="al_s", align_bytes=64)
-        nc.gpsimd.memset(al_s[:], 0)
         tab_s = keep.tile([P, T // 4], I32, name="tab_s", align_bytes=64)
         nc.sync.dma_start(tab_s[ROWS0:P, :], tab_scales[0].bitcast(I32))
-        nc.gpsimd.memset(tab_s[0:ROWS0, 0 : T // 8], 0)
-        nc.vector.memset(tab_s[0:ROWS0, T // 8 : T // 4], 0)
+        nc.vector.memset(tab_s[0:ROWS0, :], 0)
 
         v_s_words = keep.tile([P, J // 4], I32, name="v_s_words", align_bytes=64)
         nc.gpsimd.memset(v_s_words[:], 0)
         v_s = v_s_words[:].bitcast(U8).rearrange("p (b t c) -> p b t c", b=JB, t=PACK)
-
-        def load_al_scales(q):
-            nc.sync.dma_start(al_s[32 * q : 32 * q + 16, :], al_scales[:, 4 * q : 4 * q + 4, :].bitcast(I32))
-
-        for q in range(4):
-            load_al_scales(q)
 
         x_rows = x.rearrange("(p t) m -> p t m", t=PACK)
         x_first = keep.tile([P, PACK, HALF], F32, name="x_first")
@@ -77,8 +68,8 @@ def tile_list_kernl_arc_none_kernel(
 
         cols_per_pass = PASS // 16
         picked = []
-        for b0 in (0, 2):
-            picked_s = keep.tile([P, 2 * PASS], U8, name="picked_s", tag="picked%d" % b0, align_bytes=64)
+        for b0, place in ((0, 0), (2, 8448)):
+            picked_s = reuse.tile([P, 2 * PASS], U8, name="picked%d" % b0, align_bytes=64, offset=place)
             nc.vector.tensor_copy(
                 picked_s[:],
                 tab_s[:].bitcast(U8).indirect(offsets[:, b0 * cols_per_pass : (b0 + 2) * cols_per_pass]),
@@ -115,10 +106,14 @@ def tile_list_kernl_arc_none_kernel(
                 )
 
         place_scales(*picked[0])
-        x_late = keep.tile([P, PACK, HALF], F32, name="x_late", tag="picked0", align_bytes=64)
+        x_late = reuse.tile([P, PACK, HALF], F32, name="x_late", align_bytes=64, offset=256)
         nc.sync.dma_start(x_late[:], x_rows[:, :, HALF:M])
         place_scales(*picked[1])
-        al_w = keep.tile([P, JB, N], I32, name="al_w", tag="picked2", align_bytes=64)
+        al_s = reuse.tile([P, N // 4], I32, name="al_s", align_bytes=64, offset=0)
+        nc.vector.memset(al_s[:], 0)
+        for q in range(4):
+            nc.sync.dma_start(al_s[32 * q : 32 * q + 16, :], al_scales[:, 4 * q : 4 * q + 4, :].bitcast(I32))
+        al_w = reuse.tile([P, JB, N], I32, name="al_w", align_bytes=64, offset=8448)
         nc.sync.dma_start(al_w[:], al_words.rearrange("a p n i -> p a (n i)").bitcast(I32))
         quantise_x(0, x_bf[0])
         v_first = keep.tile([P, PACK, P], U32, name="v_first", align_bytes=64)

@@ -160,9 +160,16 @@ def tile_list_kernl_arc_none_kernel(
                 row = rows_of[i][:, t, :]
                 nc.vector.tensor_scalar(row, row, sign[:, b, t : t + 1], None, ALU.mult)
 
+        def by_pairs(dst, src, run):
+            return (
+                dst.rearrange("p (c i) (u e) -> p c u i e", i=run, e=2),
+                src.rearrange("p (u e) (c i) -> p c u i e", i=run, e=2),
+            )
+
         def interleave(i, c0, width, move, run):
             h_bf = ring.tile([P, width, PACK], BF16, name="h_bf", align_bytes=64)
-            move(*by_fours(h_bf[:], rows_of[i][:, :, c0 : c0 + width], run))
+            walk = by_pairs if run == 8 else by_fours
+            move(*walk(h_bf[:], rows_of[i][:, :, c0 : c0 + width], run))
             return h_bf
 
         y_half = [ypsum.tile([P, HALF], F32, name="y_half%d" % n) for n in range(NT)]

@@ -172,41 +172,54 @@ def tile_list_kernl_arc_none_kernel(
             move(*walk(h_bf[:], rows_of[i][:, :, c0 : c0 + width], run))
             return h_bf
 
-        y_half = [ypsum.tile([P, HALF], F32, name="y_half%d" % n) for n in range(NT)]
-        y_quarter = [ypsum.tile([P, NT, QUARTER], F32, name="y_quarter%d" % u) for u in range(2)]
+        def fresh_words(width):
+            return ring.tile([P, width], U32, name="h_w", align_bytes=64)[:]
 
-        def second_product(b, m0, width, h_bf):
-            h_w = ring.tile([P, width], U32, name="h_w", align_bytes=64)
+        y_half = [ypsum.tile([P, HALF], F32, name="y_half%d" % n) for n in range(NT)]
+        y_third = ypsum.tile([P, NT, QUARTER], F32, name="y_third")
+        y_fourth = [ypsum.tile([P, QUARTER], F32, name="y_fourth")]
+
+        def multiply(acc, b, n, h_w, h_s, opens, closes):
+            rows = slice(n * P, (n + 1) * P)
+            nc.tensor.matmul_mx(
+                out=acc,
+                lhsT=al_w[:, b, rows].bitcast(FP8X4),
+                lhsT_scale=al_s[:].bitcast(U8)[4 * b :, rows],
+                rhs=h_w.bitcast(FP8X4),
+                rhs_scale=h_s,
+                start=opens,
+                stop=closes,
+            )
+
+        waiting = []
+
+        def second_product(b, m0, width, h_bf, h_w):
             h_s = ring.tile([P, width], U8, name="h_s", align_bytes=64)
-            nc.vector.quantize_mx(out=h_w[:].bitcast(FP8X4), scales=h_s[:], in_=h_bf[:].rearrange("p m t -> p (m t)"))
-            y_width = HALF if m0 < HALF else QUARTER
-            for c0 in range(0, width, y_width):
+            nc.vector.quantize_mx(out=h_w.bitcast(FP8X4), scales=h_s[:], in_=h_bf.rearrange("p m t -> p (m t)"))
+            if m0 < HALF:
                 for n in range(NT):
-                    rows = slice(n * P, (n + 1) * P)
-                    if m0 < HALF:
-                        acc, opens, closes = y_half[n][:], b == 0, b == JB - 1
-                    else:
-                        acc = y_quarter[(m0 + c0 - HALF) // QUARTER][:, n, :]
-                        opens, closes = b == 0 and n == 0, b == JB - 1 and n == NT - 1
-                    nc.tensor.matmul_mx(
-                        out=acc,
-                        lhsT=al_w[:, b, rows].bitcast(FP8X4),
-                        lhsT_scale=al_s[:].bitcast(U8)[4 * b :, rows],
-                        rhs=h_w[:, c0 : c0 + y_width].bitcast(FP8X4),
-                        rhs_scale=h_s[:, c0 : c0 + y_width],
-                        start=opens,
-                        stop=closes,
-                    )
+                    multiply(y_half[n][:], b, n, h_w, h_s[:], b == 0, b == JB - 1)
+                return
+            for c0 in range(0, width, QUARTER):
+                codes, scales = h_w[:, c0 : c0 + QUARTER], h_s[:, c0 : c0 + QUARTER]
+                if m0 + c0 == HALF:
+                    for n in range(NT):
+                        multiply(y_third[:, n, :], b, n, codes, scales, b == 0 and n == 0, b == JB - 1 and n == NT - 1)
+                else:
+                    multiply(y_fourth[0][:], b, 0, codes, scales, b == 0, b == JB - 1)
+                    waiting.append((b, codes, scales))
+
+        def multiply_waiting():
+            for b, codes, scales in waiting:
+                multiply(y_fourth[1][:], b, 1, codes, scales, b == 0, b == JB - 1)
+            waiting.clear()
 
         def store_half(n):
             y_sb = keep.tile([P, HALF], F32, name="y_sb%d" % n, tag=("x_words", "early_w")[n], align_bytes=64)
             nc.scalar.copy(y_sb[:], y_half[n][:])
             nc.sync.dma_start(out[n * P : (n + 1) * P, 0:HALF], y_sb[:])
 
-        def store_quarter(u):
-            y_sb = keep.tile([P, NT, QUARTER], F32, name="y_sbq%d" % u)
-            (nc.scalar.copy, nc.vector.tensor_copy)[u](y_sb[:], y_quarter[u][:])
-            m0 = HALF + u * QUARTER
+        def store_quarter(m0, y_sb):
             nc.sync.dma_start(out[:, m0 : m0 + QUARTER].rearrange("(n p) m -> p n m", n=NT), y_sb[:])
 
         first_product(0, 0, HALF)
@@ -221,13 +234,28 @@ def tile_list_kernl_arc_none_kernel(
             apply_sign(i - 1)
             if i == 2:
                 quantise_x(1, x_bf[1])
-            if 0 <= i - 2:
-                second_product(*steps[i - 2], words_of[i - 2])
+            if 0 <= i - 2 < last - 1:
+                second_product(*steps[i - 2], words_of[i - 2][:], fresh_words(HALF))
+            if i - 2 == last - 1:
+                second_product(JB - 2, HALF, QUARTER, words_of[last - 1][:, :QUARTER, :], fresh_words(QUARTER))
             if i - 1 < last:
                 words_of[i - 1] = interleave(i - 1, 0, HALF, nc.vector.tensor_copy, 8)
-        third = interleave(last, 0, QUARTER, nc.vector.tensor_copy, 8)
+        y_fourth.append(dpsum.tile([P, QUARTER], F32, name="d"))
+        multiply_waiting()
+        third = keep.tile([P, QUARTER, PACK], BF16, name="third", align_bytes=64)
+        nc.vector.tensor_copy(*by_pairs(third[:], rows_of[last][:, :, :QUARTER], 8))
         fourth = interleave(last, QUARTER, QUARTER, nc.scalar.copy, 4)
         store_half(1)
-        for u, h_bf in enumerate((third, fourth)):
-            second_product(JB - 1, HALF + u * QUARTER, QUARTER, h_bf)
-            store_quarter(u)
+        second_product(JB - 1, HALF, QUARTER, third[:], fresh_words(QUARTER))
+        third_sb = keep.tile([P, NT, QUARTER], F32, name="third_sb")
+        nc.scalar.copy(third_sb[:], y_third[:])
+        store_quarter(HALF, third_sb)
+        late_words = keep.tile([P, QUARTER], U32, name="late_words", tag="third", align_bytes=64)
+        second_product(JB - 2, HALF + QUARTER, QUARTER, words_of[last - 1][:, QUARTER:, :], late_words[:])
+        multiply_waiting()
+        second_product(JB - 1, HALF + QUARTER, QUARTER, fourth[:], fresh_words(QUARTER))
+        multiply_waiting()
+        fourth_sb = keep.tile([P, NT, QUARTER], F32, name="fourth_sb")
+        nc.scalar.copy(fourth_sb[:, 0, :], y_fourth[0][:])
+        nc.vector.tensor_copy(fourth_sb[:, 1, :], y_fourth[1][:])
+        store_quarter(HALF + QUARTER, fourth_sb)

@@ -134,7 +134,10 @@ def tile_list_kernl_arc_none_kernel(
             b, m0, step_width = steps[i]
             cols = slice(m0 + c0, m0 + c0 + width)
             if c0 == 0:
-                rows_of[i] = ring.tile([P, PACK, step_width], BF16, name="h_rows", align_bytes=64)
+                if i < len(steps) - 1:
+                    rows_of[i] = ring.tile([P, PACK, step_width], BF16, name="h_rows", align_bytes=64)
+                else:
+                    rows_of[i] = keep.tile([P, PACK, step_width], BF16, name="last_rows", align_bytes=64)
             for t in range(PACK):
                 d = dpsum.tile([P, width], F32, name="d")
                 nc.tensor.matmul_mx(
@@ -215,7 +218,7 @@ def tile_list_kernl_arc_none_kernel(
             waiting.clear()
 
         def store_half(n):
-            y_sb = keep.tile([P, HALF], F32, name="y_sb%d" % n, tag=("x_words", "early_w")[n], align_bytes=64)
+            y_sb = keep.tile([P, HALF], F32, name="y_sb%d" % n, tag=("x_words", "last_rows")[n], align_bytes=64)
             nc.scalar.copy(y_sb[:], y_half[n][:])
             nc.sync.dma_start(out[n * P : (n + 1) * P, 0:HALF], y_sb[:])
 

@@ -120,6 +120,8 @@ def tile_list_kernl_arc_none_kernel(
         gather_words(0, v_first[:])
         nc.scalar.activation(mag[:], cw_sb[:], ACT.Abs)
         nc.scalar.activation(sign[:], cw_sb[:], ACT.Sign)
+        last_mag = reuse.tile([P, 1], F32, name="last_mag", align_bytes=64, offset=12544)
+        nc.scalar.activation(last_mag[:], cw_sb[:, JB - 1, PACK - 1 : PACK], ACT.Abs)
         nc.vector.tensor_tensor(bias[:], mag[:], cb_sb[:], ALU.mult)
         v_rest = keep.tile([P, JB - 1, PACK, P], U32, name="v_rest", tag="early_w", align_bytes=64)
         for b in range(1, JB):
@@ -134,10 +136,7 @@ def tile_list_kernl_arc_none_kernel(
             b, m0, step_width = steps[i]
             cols = slice(m0 + c0, m0 + c0 + width)
             if c0 == 0:
-                if i < len(steps) - 1:
-                    rows_of[i] = ring.tile([P, PACK, step_width], BF16, name="h_rows", align_bytes=64)
-                else:
-                    rows_of[i] = keep.tile([P, PACK, step_width], BF16, name="last_rows", align_bytes=64)
+                rows_of[i] = ring.tile([P, PACK, step_width], BF16, name="h_rows", align_bytes=64)
             for t in range(PACK):
                 d = dpsum.tile([P, width], F32, name="d")
                 nc.tensor.matmul_mx(
@@ -154,7 +153,7 @@ def tile_list_kernl_arc_none_kernel(
                     d[:],
                     ACT.Relu,
                     bias=bias[:, b, t : t + 1],
-                    scale=mag[:, b, t : t + 1],
+                    scale=last_mag[:] if (i, t) == (len(steps) - 1, PACK - 1) else mag[:, b, t : t + 1],
                 )
 
         def apply_sign(i):
@@ -179,8 +178,7 @@ def tile_list_kernl_arc_none_kernel(
             return ring.tile([P, width], U32, name="h_w", align_bytes=64)[:]
 
         y_half = [ypsum.tile([P, HALF], F32, name="y_half%d" % n) for n in range(NT)]
-        y_third = ypsum.tile([P, NT, QUARTER], F32, name="y_third")
-        y_fourth = [ypsum.tile([P, QUARTER], F32, name="y_fourth")]
+        y_late = {(u, 0): ypsum.tile([P, QUARTER], F32, name="y_late%d" % u) for u in range(2)}
 
         def multiply(acc, b, n, h_w, h_s, opens, closes):
             rows = slice(n * P, (n + 1) * P)
@@ -205,24 +203,27 @@ def tile_list_kernl_arc_none_kernel(
                 return
             for c0 in range(0, width, QUARTER):
                 codes, scales = h_w[:, c0 : c0 + QUARTER], h_s[:, c0 : c0 + QUARTER]
-                if m0 + c0 == HALF:
-                    for n in range(NT):
-                        multiply(y_third[:, n, :], b, n, codes, scales, b == 0 and n == 0, b == JB - 1 and n == NT - 1)
-                else:
-                    multiply(y_fourth[0][:], b, 0, codes, scales, b == 0, b == JB - 1)
-                    waiting.append((b, codes, scales))
+                u = (m0 + c0 - HALF) // QUARTER
+                multiply(y_late[u, 0][:], b, 0, codes, scales, b == 0, b == JB - 1)
+                waiting.append((u, b, codes, scales))
+            if (0, 1) in y_late:
+                multiply_waiting()
 
         def multiply_waiting():
-            for b, codes, scales in waiting:
-                multiply(y_fourth[1][:], b, 1, codes, scales, b == 0, b == JB - 1)
+            for u, b, codes, scales in waiting:
+                multiply(y_late[u, 1][:], b, 1, codes, scales, b == 0, b == JB - 1)
             waiting.clear()
 
         def store_half(n):
-            y_sb = keep.tile([P, HALF], F32, name="y_sb%d" % n, tag=("x_words", "last_rows")[n], align_bytes=64)
+            y_sb = keep.tile([P, HALF], F32, name="y_sb%d" % n, tag=("x_words", "early_w")[n], align_bytes=64)
             nc.scalar.copy(y_sb[:], y_half[n][:])
             nc.sync.dma_start(out[n * P : (n + 1) * P, 0:HALF], y_sb[:])
 
-        def store_quarter(m0, y_sb):
+        def store_quarter(u):
+            y_sb = keep.tile([P, NT, QUARTER], F32, name="y_sbq%d" % u)
+            nc.scalar.copy(y_sb[:, 0, :], y_late[u, 0][:])
+            nc.vector.tensor_copy(y_sb[:, 1, :], y_late[u, 1][:])
+            m0 = HALF + u * QUARTER
             nc.sync.dma_start(out[:, m0 : m0 + QUARTER].rearrange("(n p) m -> p n m", n=NT), y_sb[:])
 
         first_product(0, 0, HALF)
@@ -240,25 +241,18 @@ def tile_list_kernl_arc_none_kernel(
             if 0 <= i - 2 < last - 1:
                 second_product(*steps[i - 2], words_of[i - 2][:], fresh_words(HALF))
             if i - 2 == last - 1:
-                second_product(JB - 2, HALF, QUARTER, words_of[last - 1][:, :QUARTER, :], fresh_words(QUARTER))
+                for u in range(2):
+                    y_late[u, 1] = dpsum.tile([P, QUARTER], F32, name="d")
+                multiply_waiting()
+                held_words = reuse.tile([P, HALF], U32, name="held_words", align_bytes=64, offset=12544)
+                second_product(JB - 2, HALF, QUARTER, words_of[last - 1][:, :QUARTER, :], held_words[:, :QUARTER])
             if i - 1 < last:
                 words_of[i - 1] = interleave(i - 1, 0, HALF, nc.vector.tensor_copy, 8)
-        y_fourth.append(dpsum.tile([P, QUARTER], F32, name="d"))
-        multiply_waiting()
-        third = keep.tile([P, QUARTER, PACK], BF16, name="third", align_bytes=64)
-        nc.vector.tensor_copy(*by_pairs(third[:], rows_of[last][:, :, :QUARTER], 8))
+        third = interleave(last, 0, QUARTER, nc.vector.tensor_copy, 8)
         fourth = interleave(last, QUARTER, QUARTER, nc.scalar.copy, 4)
         store_half(1)
+        second_product(JB - 2, HALF + QUARTER, QUARTER, words_of[last - 1][:, QUARTER:, :], held_words[:, QUARTER:])
         second_product(JB - 1, HALF, QUARTER, third[:], fresh_words(QUARTER))
-        third_sb = keep.tile([P, NT, QUARTER], F32, name="third_sb")
-        nc.scalar.copy(third_sb[:], y_third[:])
-        store_quarter(HALF, third_sb)
-        late_words = keep.tile([P, QUARTER], U32, name="late_words", tag="third", align_bytes=64)
-        second_product(JB - 2, HALF + QUARTER, QUARTER, words_of[last - 1][:, QUARTER:, :], late_words[:])
-        multiply_waiting()
         second_product(JB - 1, HALF + QUARTER, QUARTER, fourth[:], fresh_words(QUARTER))
-        multiply_waiting()
-        fourth_sb = keep.tile([P, NT, QUARTER], F32, name="fourth_sb")
-        nc.scalar.copy(fourth_sb[:, 0, :], y_fourth[0][:])
-        nc.vector.tensor_copy(fourth_sb[:, 1, :], y_fourth[1][:])
-        store_quarter(HALF + QUARTER, fourth_sb)
+        for u in range(2):
+            store_quarter(u)

@@ -215,7 +215,7 @@ def tile_list_kernl_arc_none_kernel(
             waiting.clear()
 
         def store_half(n):
-            y_sb = keep.tile([P, HALF], F32, name="y_sb%d" % n, tag=("x_words", "early_w")[n], align_bytes=64)
+            y_sb = keep.tile([P, HALF], F32, name="y_sb%d" % n, tag=("v_first", "early_w")[n], align_bytes=64)
             nc.scalar.copy(y_sb[:], y_half[n][:])
             nc.sync.dma_start(out[n * P : (n + 1) * P, 0:HALF], y_sb[:])
 
@@ -233,8 +233,8 @@ def tile_list_kernl_arc_none_kernel(
         for i in range(1, last + 2):
             if i <= last:
                 first_product(i, 0, HALF)
-            if i == last:
-                store_half(0)
+            if last - 1 <= i <= last:
+                store_half(i - last + 1)
             apply_sign(i - 1)
             if i == 2:
                 quantise_x(1, x_bf[1])
@@ -250,7 +250,6 @@ def tile_list_kernl_arc_none_kernel(
                 words_of[i - 1] = interleave(i - 1, 0, HALF, nc.vector.tensor_copy, 8)
         third = interleave(last, 0, QUARTER, nc.vector.tensor_copy, 8)
         fourth = interleave(last, QUARTER, QUARTER, nc.scalar.copy, 4)
-        store_half(1)
         second_product(JB - 2, HALF + QUARTER, QUARTER, words_of[last - 1][:, QUARTER:, :], held_words[:, QUARTER:])
         second_product(JB - 1, HALF, QUARTER, third[:], fresh_words(QUARTER))
         second_product(JB - 1, HALF + QUARTER, QUARTER, fourth[:], fresh_words(QUARTER))

@@ -121,7 +121,7 @@ def tile_list_kernl_arc_none_kernel(
         nc.scalar.activation(mag[:], cw_sb[:], ACT.Abs)
         nc.scalar.activation(sign[:], cw_sb[:], ACT.Sign)
         last_mag = reuse.tile([P, 1], F32, name="last_mag", align_bytes=64, offset=12544)
-        nc.scalar.activation(last_mag[:], cw_sb[:, JB - 1, PACK - 1 : PACK], ACT.Abs)
+        nc.scalar.copy(last_mag[:], mag[:, JB - 1, PACK - 1 : PACK])
         nc.vector.tensor_tensor(bias[:], mag[:], cb_sb[:], ALU.mult)
         v_rest = keep.tile([P, JB - 1, PACK, P], U32, name="v_rest", tag="early_w", align_bytes=64)
         for b in range(1, JB):
@@ -249,9 +249,12 @@ def tile_list_kernl_arc_none_kernel(
             if i - 1 < last:
                 words_of[i - 1] = interleave(i - 1, 0, HALF, nc.vector.tensor_copy, 8)
         third = interleave(last, 0, QUARTER, nc.vector.tensor_copy, 8)
-        fourth = interleave(last, QUARTER, QUARTER, nc.scalar.copy, 4)
-        second_product(JB - 2, HALF + QUARTER, QUARTER, words_of[last - 1][:, QUARTER:, :], held_words[:, QUARTER:])
+        fourth = ring.tile([P, QUARTER, PACK], BF16, name="h_bf", align_bytes=64)
+        split = QUARTER // 4
+        nc.vector.tensor_copy(*by_pairs(fourth[:, :split, :], rows_of[last][:, :, QUARTER : QUARTER + split], 8))
+        nc.scalar.copy(*by_fours(fourth[:, split:, :], rows_of[last][:, :, QUARTER + split :], 4))
         second_product(JB - 1, HALF, QUARTER, third[:], fresh_words(QUARTER))
+        second_product(JB - 2, HALF + QUARTER, QUARTER, words_of[last - 1][:, QUARTER:, :], held_words[:, QUARTER:])
         second_product(JB - 1, HALF + QUARTER, QUARTER, fourth[:], fresh_words(QUARTER))
         for u in range(2):
             store_quarter(u)

from contextlib import ExitStack

import concourse.mybir as mybir

K, M, N, J, T = 512, 1024, 256, 2048, 4096
FLOPS = 2 * K * M * J + 2 * J * M * N

F32 = mybir.dt.float32
BF16 = mybir.dt.bfloat16
I32 = mybir.dt.int32
U32 = mybir.dt.uint32
U16 = mybir.dt.uint16
U8 = mybir.dt.uint8
FP8X4 = mybir.dt.float8_e4m3fn_x4
ALU = mybir.AluOpType
ACT = mybir.ActivationFunctionType

P = 128
PACK = 4
PASS = P * PACK
JB = J // PASS
HALF = 512
HALVES = M // HALF
QUARTER = 256
NT = N // P
SHARE = 256
ROWS0 = P - 16


def tile_list_kernl_arc_none_kernel(
    tc, x, tab_words, tab_scales, cw, cb, al_words, al_scales, offs, out
):
    nc = tc.nc
    with ExitStack() as ctx:
        keep = ctx.enter_context(tc.tile_pool(name="keep", bufs=1))
        ring = ctx.enter_context(tc.tile_pool(name="ring", bufs=4))
        reuse = ctx.enter_context(tc.tile_pool(name="reuse", bufs=1))
        dpsum = ctx.enter_context(tc.psum_pool(name="dpsum", bufs=4))
        ypsum = ctx.enter_context(tc.psum_pool(name="ypsum", bufs=1))

        offsets = keep.tile([P, J // 16], U16, name="offsets")
        nc.sync.dma_start(offsets[:], offs)

        tab_s = keep.tile([P, T // 4], I32, name="tab_s", align_bytes=64)
        nc.sync.dma_start(tab_s[ROWS0:P, :], tab_scales[0].bitcast(I32))
        nc.vector.memset(tab_s[0:ROWS0, :], 0)

        v_s_words = keep.tile([P, J // 4], I32, name="v_s_words", align_bytes=64)
        nc.gpsimd.memset(v_s_words[:], 0)
        v_s = v_s_words[:].bitcast(U8).rearrange("p (b t c) -> p b t c", b=JB, t=PACK)

        x_rows = x.rearrange("(p t) m -> p t m", t=PACK)
        x_first = keep.tile([P, PACK, HALF], F32, name="x_first")
        nc.sync.dma_start(x_first[:], x_rows[:, :, 0:HALF])
        tab_w = keep.tile([P, T], I32, name="tab_w", align_bytes=64)
        nc.sync.dma_start(tab_w[:], tab_words[0].rearrange("p t i -> p (t i)").bitcast(I32))
        cw_sb = keep.tile([P, JB, PACK], F32, name="cw_sb", tag="early_w", align_bytes=64)
        cb_sb = keep.tile([P, JB, PACK], F32, name="cb_sb")
        nc.sync.dma_start(cb_sb[:], cb.rearrange("(b p t) -> p b t", b=JB, t=PACK))
        nc.sync.dma_start(cw_sb[:], cw.rearrange("(b p t) -> p b t", b=JB, t=PACK))

        sign = keep.tile([P, JB, PACK], F32, name="sign")
        mag = keep.tile([P, JB, PACK], F32, name="mag")
        bias = keep.tile([P, JB, PACK], F32, name="bias")

        x_w = keep.tile([P, M], U32, name="x_w", tag="x_words", align_bytes=64)
        x_s = keep.tile([P, M], U8, name="x_s", align_bytes=64)

        cols_per_pass = PASS // 16
        picked = []
        for b0, place in ((0, 0), (2, 8448)):
            picked_s = reuse.tile([P, 2 * PASS], U8, name="picked%d" % b0, align_bytes=64, offset=place)
            nc.vector.tensor_copy(
                picked_s[:],
                tab_s[:].bitcast(U8).indirect(offsets[:, b0 * cols_per_pass : (b0 + 2) * cols_per_pass]),
            )
            picked.append((b0, picked_s))

        def by_fours(dst, src, run=4):
            return dst.rearrange("p (c i) t -> p c t i", i=run), src.rearrange("p t (c i) -> p c t i", i=run)

        def quantise_x(h, x_bf):
            cols = slice(h * HALF, (h + 1) * HALF)
            nc.vector.quantize_mx(
                out=x_w[:, cols].bitcast(FP8X4), scales=x_s[:, cols], in_=x_bf[:].rearrange("p m t -> p (m t)")
            )

        def gather_words(b, dst):
            nc.vector.tensor_copy(
                dst.rearrange("p t c -> p c t"),
                tab_w[:].bitcast(U32).indirect(offsets[:, b * cols_per_pass : (b + 1) * cols_per_pass]),
            )

        x_bf = [keep.tile([P, HALF, PACK], BF16, name="x_bf%d" % h, align_bytes=64) for h in range(HALVES)]
        nc.scalar.activation(*by_fours(x_bf[0][:], x_first[:]), ACT.Copy)

        def place_scales(b0, picked_s):
            by_slot = keep.tile([P, 2 * P], I32, name="by_slot%d" % b0, align_bytes=64)
            nc.vector.tensor_copy(
                by_slot[:].bitcast(U8).rearrange("p (b t c) -> p b t c", b=2, t=PACK),
                picked_s[:].rearrange("p (b c t) -> p b t c", b=2, t=PACK),
            )
            for q in range(4):
                nc.sync.dma_start(
                    v_s_words[32 * q : 32 * q + 4, b0 * P : (b0 + 2) * P], by_slot[ROWS0 + 4 * q : ROWS0 + 4 * q + 4, :]
                )

        place_scales(*picked[0])
        x_late = reuse.tile([P, PACK, HALF], F32, name="x_late", align_bytes=64, offset=256)
        nc.sync.dma_start(x_late[:], x_rows[:, :, HALF:M])
        place_scales(*picked[1])
        al_s = reuse.tile([P, N // 4], I32, name="al_s", align_bytes=64, offset=0)
        nc.vector.memset(al_s[:], 0)
        for q in range(4):
            nc.sync.dma_start(al_s[32 * q : 32 * q + 16, :], al_scales[:, 4 * q : 4 * q + 4, :].bitcast(I32))
        al_w = reuse.tile([P, JB, N], I32, name="al_w", align_bytes=64, offset=8448)
        nc.sync.dma_start(al_w[:], al_words.rearrange("a p n i -> p a (n i)").bitcast(I32))
        quantise_x(0, x_bf[0])
        v_first = keep.tile([P, PACK, P], U32, name="v_first", align_bytes=64)
        gather_words(0, v_first[:])
        nc.scalar.activation(mag[:], cw_sb[:], ACT.Abs)
        nc.scalar.activation(sign[:], cw_sb[:], ACT.Sign)
        last_mag = reuse.tile([P, 1], F32, name="last_mag", align_bytes=64, offset=12544)
        nc.scalar.copy(last_mag[:], mag[:, JB - 1, PACK - 1 : PACK])
        nc.vector.tensor_tensor(bias[:], mag[:], cb_sb[:], ALU.mult)
        v_rest = keep.tile([P, JB - 1, PACK, P], U32, name="v_rest", tag="early_w", align_bytes=64)
        for b in range(1, JB):
            gather_words(b, v_rest[:, b - 1])
        v_w = [v_first[:]] + [v_rest[:, b] for b in range(JB - 1)]
        nc.vector.tensor_copy(*by_fours(x_bf[1][:, SHARE:, :], x_late[:, :, SHARE:]))

        steps = [(b, m0, HALF) for m0 in range(0, M, HALF) for b in range(JB)]
        rows_of = {}

        def first_product(i, c0, width):
            b, m0, step_width = steps[i]
            cols = slice(m0 + c0, m0 + c0 + width)
            if c0 == 0:
                rows_of[i] = ring.tile([P, PACK, step_width], BF16, name="h_rows", align_bytes=64)
            for t in range(PACK):
                d = dpsum.tile([P, width], F32, name="d")
                nc.tensor.matmul_mx(
                    out=d[:],
                    lhsT=v_w[b][:, t, :].bitcast(FP8X4),
                    lhsT_scale=v_s[:, b, t, :],
                    rhs=x_w[:, cols].bitcast(FP8X4),
                    rhs_scale=x_s[:, cols],
                    start=True,
                    stop=True,
                )
                nc.scalar.activation(
                    rows_of[i][:, t, c0 : c0 + width],
                    d[:],
                    ACT.Relu,
                    bias=bias[:, b, t : t + 1],
                    scale=last_mag[:] if (i, t) == (len(steps) - 1, PACK - 1) else mag[:, b, t : t + 1],
                )

        def apply_sign(i):
            b = steps[i][0]
            for t in range(PACK):
                row = rows_of[i][:, t, :]
                nc.vector.tensor_scalar(row, row, sign[:, b, t : t + 1], None, ALU.mult)

        def by_pairs(dst, src, run):
            return (
                dst.rearrange("p (c i) (u e) -> p c u i e", i=run, e=2),
                src.rearrange("p (u e) (c i) -> p c u i e", i=run, e=2),
            )

        def interleave(i, c0, width, move, run):
            h_bf = ring.tile([P, width, PACK], BF16, name="h_bf", align_bytes=64)
            walk = by_pairs if run == 8 else by_fours
            move(*walk(h_bf[:], rows_of[i][:, :, c0 : c0 + width], run))
            return h_bf

        def fresh_words(width):
            return ring.tile([P, width], U32, name="h_w", align_bytes=64)[:]

        y_half = [ypsum.tile([P, HALF], F32, name="y_half%d" % n) for n in range(NT)]
        y_late = {(u, 0): ypsum.tile([P, QUARTER], F32, name="y_late%d" % u) for u in range(2)}

        def multiply(acc, b, n, h_w, h_s, opens, closes):
            rows = slice(n * P, (n + 1) * P)
            nc.tensor.matmul_mx(
                out=acc,
                lhsT=al_w[:, b, rows].bitcast(FP8X4),
                lhsT_scale=al_s[:].bitcast(U8)[4 * b :, rows],
                rhs=h_w.bitcast(FP8X4),
                rhs_scale=h_s,
                start=opens,
                stop=closes,
            )

        waiting = []

        def second_product(b, m0, width, h_bf, h_w):
            h_s = ring.tile([P, width], U8, name="h_s", align_bytes=64)
            nc.vector.quantize_mx(out=h_w.bitcast(FP8X4), scales=h_s[:], in_=h_bf.rearrange("p m t -> p (m t)"))
            if m0 < HALF:
                for n in range(NT):
                    multiply(y_half[n][:], b, n, h_w, h_s[:], b == 0, b == JB - 1)
                return
            for c0 in range(0, width, QUARTER):
                codes, scales = h_w[:, c0 : c0 + QUARTER], h_s[:, c0 : c0 + QUARTER]
                u = (m0 + c0 - HALF) // QUARTER
                multiply(y_late[u, 0][:], b, 0, codes, scales, b == 0, b == JB - 1)
                waiting.append((u, b, codes, scales))
            if (0, 1) in y_late:
                multiply_waiting()

        def multiply_waiting():
            for u, b, codes, scales in waiting:
                multiply(y_late[u, 1][:], b, 1, codes, scales, b == 0, b == JB - 1)
            waiting.clear()

        def store_half(n):
            y_sb = keep.tile([P, HALF], F32, name="y_sb%d" % n, tag=("v_first", "early_w")[n], align_bytes=64)
            nc.scalar.copy(y_sb[:], y_half[n][:])
            nc.sync.dma_start(out[n * P : (n + 1) * P, 0:HALF], y_sb[:])

        def store_quarter(u):
            y_sb = keep.tile([P, NT, QUARTER], F32, name="y_sbq%d" % u)
            nc.scalar.copy(y_sb[:, 0, :], y_late[u, 0][:])
            nc.vector.tensor_copy(y_sb[:, 1, :], y_late[u, 1][:])
            m0 = HALF + u * QUARTER
            nc.sync.dma_start(out[:, m0 : m0 + QUARTER].rearrange("(n p) m -> p n m", n=NT), y_sb[:])

        first_product(0, 0, HALF)
        nc.scalar.activation(*by_fours(x_bf[1][:, :SHARE, :], x_late[:, :, :SHARE]), ACT.Copy)
        words_of = {}
        last = len(steps) - 1
        for i in range(1, last + 2):
            if i <= last:
                first_product(i, 0, HALF)
            if last - 1 <= i <= last:
                store_half(i - last + 1)
            apply_sign(i - 1)
            if i == 2:
                quantise_x(1, x_bf[1])
            if 0 <= i - 2 < last - 1:
                second_product(*steps[i - 2], words_of[i - 2][:], fresh_words(HALF))
            if i - 2 == last - 1:
                for u in range(2):
                    y_late[u, 1] = dpsum.tile([P, QUARTER], F32, name="d")
                multiply_waiting()
                held_words = reuse.tile([P, HALF], U32, name="held_words", align_bytes=64, offset=12544)
                second_product(JB - 2, HALF, QUARTER, words_of[last - 1][:, :QUARTER, :], held_words[:, :QUARTER])
            if i - 1 < last:
                words_of[i - 1] = interleave(i - 1, 0, HALF, nc.vector.tensor_copy, 8)
        third = interleave(last, 0, QUARTER, nc.vector.tensor_copy, 8)
        fourth = ring.tile([P, QUARTER, PACK], BF16, name="h_bf", align_bytes=64)
        split = QUARTER // 4
        nc.vector.tensor_copy(*by_pairs(fourth[:, :split, :], rows_of[last][:, :, QUARTER : QUARTER + split], 8))
        nc.scalar.copy(*by_fours(fourth[:, split:, :], rows_of[last][:, :, QUARTER + split :], 4))
        second_product(JB - 1, HALF, QUARTER, third[:], fresh_words(QUARTER))
        second_product(JB - 2, HALF + QUARTER, QUARTER, words_of[last - 1][:, QUARTER:, :], held_words[:, QUARTER:])
        second_product(JB - 1, HALF + QUARTER, QUARTER, fourth[:], fresh_words(QUARTER))
        for u in range(2):
            store_quarter(u)
